import numpy as np
import ml_dtypes


def mxq(x, axis, fmt="e4m3"):
    dtype, down = {"e4m3": (ml_dtypes.float8_e4m3fn, 7), "e5m2": (ml_dtypes.float8_e5m2, 14)}[fmt]
    v = np.moveaxis(np.asarray(x, np.float32).astype(ml_dtypes.bfloat16).astype(np.float64), axis, -1)
    blocks = v.reshape(v.shape[:-1] + (-1, 32))
    amax = np.abs(blocks).max(-1, keepdims=True)
    byte = np.maximum(np.where(amax > 0, np.frexp(amax)[1] - 1 + 127, 0) - down, 1)
    scale = np.exp2(byte - 127.0)
    codes = (blocks / scale).astype(np.float32).astype(dtype).astype(np.float64)
    return np.moveaxis((codes * scale).reshape(v.shape), -1, axis)


WIDE = False


def mx_kscale(k):
    if not WIDE:
        return np.ones(k)
    levels = np.array([10, -10, 5, -5, 0])
    if k % 512:
        return np.exp2(np.random.permutation(np.resize(levels, k // 32))).repeat(32)
    a = np.empty((k // 512, 16))
    for p in range(k // 512):
        a[p, :8] = np.random.permutation(np.resize(levels, 8))
        for g in range(8):
            far = levels[np.abs(levels - a[p, g]) >= 10]
            a[p, g + 8] = far[np.random.randint(len(far))]
    return np.exp2(a.ravel()).repeat(32)


def f64(x):
    return np.asarray(x).astype(np.float64)


def striped(idx):
    return np.tile(idx.reshape(-1, 16).T, (8, 1)).astype(np.uint16)


def unstriped(offs):
    return offs[:16].T.reshape(-1).astype(np.int64)


def pack_weight(w):
    k, n = w.shape
    w = f64(np.asarray(w, np.float32).astype(ml_dtypes.bfloat16)).reshape(k // 32, 32, n)
    amax = np.abs(w).max(1)
    byte = np.clip(np.where(amax > 0, np.frexp(amax)[1] - 1 + 127 - 7, 1), 1, 254)
    scaled = (w * np.exp2(127.0 - byte)[:, None, :]).reshape(k, n).astype(np.float32)
    words = np.ascontiguousarray(scaled.reshape(k // 512, 128, 4, n).transpose(0, 1, 3, 2)).astype(ml_dtypes.float8_e4m3fn).view(np.uint8)
    return words, np.ascontiguousarray(byte.astype(np.uint8).reshape(k // 512, 16, n))


def unpack_weight(words, scales):
    g, p, n, _ = words.shape
    vals = np.ascontiguousarray(words).view(ml_dtypes.float8_e4m3fn).astype(np.float64) * np.repeat(np.exp2(scales.astype(np.float64) - 127.0), 8, axis=1)[..., None]
    return vals.transpose(0, 1, 3, 2).reshape(g * 512, n)


def gelu(v):
    return 0.5 * v * (1.0 + np.tanh(np.sqrt(2.0 / np.pi) * (v + 0.044715 * v**3)))


K, T, S, D, H, V, G, R = 1024, 2048, 512, 8, 512, 1024, 4096, 128


def setup_inputs():
    n = np.random.standard_normal
    s = mx_kscale(K)[:, None]
    u = mx_kscale(H)
    packed_xT = pack_weight(n((K, T)) * s)
    packed_vT = pack_weight(n((H, G)) / np.sqrt(H) / u[:, None])
    return {
        "x_words": packed_xT[0],
        "x_scales": packed_xT[1],
        "w1": (n((K, H)) / np.sqrt(K) / s * u).astype(np.float32),
        "v_words": packed_vT[0],
        "v_scales": packed_vT[1],
        "offs": striped(np.random.permutation(T)[:S]),
        "doc": striped(np.random.permutation(G)[:V]),
    }


def reference(x_words, x_scales, w1, v_words, v_scales, offs, doc):
    xq = unpack_weight(x_words, x_scales)[:, unstriped(offs)]
    h = gelu(mxq(f64(w1), 0, "e4m3").T @ xq)
    v_doc = unpack_weight(v_words, v_scales)[:, unstriped(doc)]
    y = mxq(h, 0, "e4m3").T @ v_doc
    return y.reshape(H, R, D).max(axis=2)

@@ -1,0 +1,149 @@
+from contextlib import ExitStack
+
+import concourse.mybir as mybir
+
+K, T, S, D, H, V, G, R = 1024, 2048, 512, 8, 512, 1024, 4096, 128
+FLOPS = 2 * K * H * S + 2 * H * S * V
+
+F32 = mybir.dt.float32
+BF16 = mybir.dt.bfloat16
+I32 = mybir.dt.int32
+U32 = mybir.dt.uint32
+U16 = mybir.dt.uint16
+U8 = mybir.dt.uint8
+FP8X4 = mybir.dt.float8_e4m3fn_x4
+GELU = mybir.ActivationFunctionType.Gelu_apprx_tanh
+MAX = mybir.AluOpType.max
+AXIS_X = mybir.AxisListType.X
+
+P = 128
+PACK = 4
+K_PASS = P * PACK
+PASSES = K // K_PASS
+QUADS = 4
+QUAD = 32
+ROWS = 4
+V_ROW0 = 8
+BANK = 512
+LIST = 16
+
+
+def tile_picked_zlateq_gelu_p_kernel(tc, x_words, x_scales, w1, v_words, v_scales, offs, doc, out):
+    nc = tc.nc
+    with ExitStack() as ctx:
+        keep = ctx.enter_context(tc.tile_pool(name="keep", bufs=1))
+        psum = ctx.enter_context(tc.psum_pool(name="psum", bufs=8))
+
+        offs_t = keep.tile([P, S // LIST], U16, name="offs_t")
+        doc_t = keep.tile([P, V // LIST], U16, name="doc_t")
+        xs_tab = keep.tile([P, T], U8, name="xs_tab", align_bytes=64)
+        vs_tab = keep.tile([P, G], U8, name="vs_tab", align_bytes=64)
+        xw_tab = [keep.tile([P, T], I32, name="xw_tab%d" % o, align_bytes=64) for o in range(PASSES)]
+        vw_tab = keep.tile([P, G], I32, name="vw_tab", align_bytes=64)
+        w_raw = [keep.tile([P, PACK, H], F32, name="w_raw%d" % o, align_bytes=64) for o in range(PASSES)]
+
+        def load_w(o):
+            nc.sync.dma_start(out=w_raw[o][:], in_=w1[o * K_PASS : (o + 1) * K_PASS, :].rearrange("(p j) c -> p j c", j=PACK))
+
+        def load_words(tab, words):
+            nc.sync.dma_start(out=tab[:], in_=words.rearrange("p n t -> p (n t)").bitcast(I32))
+
+        nc.vector.memset(xs_tab[:].bitcast(I32), 0)
+        nc.gpsimd.memset(vs_tab[:].bitcast(I32), 0)
+        load_w(0)
+        for q in range(QUADS):
+            nc.sync.dma_start(
+                out=xs_tab[QUAD * q : QUAD * q + PASSES * ROWS, :].bitcast(I32),
+                in_=x_scales[:, ROWS * q : ROWS * (q + 1), :].bitcast(I32),
+            )
+        nc.sync.dma_start(offs_t[:], offs)
+        nc.sync.dma_start(doc_t[:], doc)
+        for q in range(QUADS):
+            nc.gpsimd.dma_start(
+                out=vs_tab[QUAD * q + V_ROW0 : QUAD * q + V_ROW0 + ROWS, :].bitcast(I32),
+                in_=v_scales[0, ROWS * q : ROWS * (q + 1), :].bitcast(I32),
+            )
+        load_w(1)
+        load_words(xw_tab[0], x_words[0])
+        load_words(xw_tab[1], x_words[1])
+        load_words(vw_tab, v_words[0])
+
+        xs = keep.tile([P, S], U8, name="xs", align_bytes=64)
+        vs = keep.tile([P, V], U8, name="vs", align_bytes=64)
+        nc.vector.tensor_copy(xs[:], xs_tab[:].indirect(offs_t[:]))
+        nc.vector.tensor_copy(vs[:], vs_tab[:].indirect(doc_t[:]))
+
+        w_codes, w_scales = [], []
+        for o in range(PASSES):
+            grouped = keep.tile([P, H * PACK], BF16, name="w_grouped%d" % o, align_bytes=64)
+            dst = grouped[:].rearrange("p (t m j) -> p m j t", t=PACK, j=PACK)
+            src = w_raw[o][:].rearrange("p j (m t) -> p m j t", t=PACK)
+            if o == 0:
+                nc.scalar.copy(dst, src)
+            else:
+                nc.vector.tensor_copy(dst, src)
+            codes = keep.tile([P, H], U32, name="w_codes%d" % o, align_bytes=64)
+            scales = keep.tile([P, H], U8, name="w_scales%d" % o, align_bytes=64)
+            nc.vector.quantize_mx(out=codes[:].bitcast(FP8X4), scales=scales[:], in_=grouped[:])
+            w_codes.append(codes)
+            w_scales.append(scales)
+
+        xw = [keep.tile([P, S], U32, name="xw%d" % o, align_bytes=64) for o in range(PASSES)]
+        nc.vector.tensor_copy(xw[0][:], xw_tab[0][:].bitcast(U32).indirect(offs_t[:]))
+        half = S // 2
+        for a in range(2):
+            nc.vector.tensor_copy(
+                xw[1][:, a * half : (a + 1) * half],
+                xw_tab[1][:].bitcast(U32).indirect(offs_t[:, a * half // LIST : (a + 1) * half // LIST]),
+            )
+
+        h_codes, h_scales = [], []
+        for b in range(S // P):
+            tok = slice(b * P, (b + 1) * P)
+            acc = psum.tile([P, BANK], F32, name="acc")
+            for t in range(PACK):
+                ch = slice(t * P, (t + 1) * P)
+                for o in range(PASSES):
+                    nc.tensor.matmul_mx(
+                        out=acc[:, ch],
+                        lhsT=w_codes[o][:, ch].bitcast(FP8X4),
+                        lhsT_scale=w_scales[o][:, ch],
+                        rhs=xw[o][:, tok].bitcast(FP8X4),
+                        rhs_scale=xs[ROWS * o : P, tok],
+                        start=(o == 0),
+                        stop=(o == PASSES - 1),
+                    )
+            h_bf = keep.tile([P, P * PACK], BF16, name="h_bf%d" % b, align_bytes=64)
+            nc.scalar.activation(
+                h_bf[:].rearrange("p (n t) -> p n t", t=PACK), acc[:].rearrange("p (t n) -> p n t", t=PACK), GELU
+            )
+            codes = keep.tile([P, P], U32, name="h_codes%d" % b, align_bytes=64)
+            scales = keep.tile([P, P], U8, name="h_scales%d" % b, align_bytes=64)
+            nc.vector.quantize_mx(out=codes[:].bitcast(FP8X4), scales=scales[:], in_=h_bf[:])
+            h_codes.append(codes)
+            h_scales.append(scales)
+
+        vw = [keep.tile([P, BANK], U32, name="vw%d" % g, align_bytes=64) for g in range(V // BANK)]
+        for g in range(V // BANK):
+            nc.vector.tensor_copy(
+                vw[g][:], vw_tab[:].bitcast(U32).indirect(doc_t[:, g * BANK // LIST : (g + 1) * BANK // LIST])
+            )
+        best = [keep.tile([P, R], F32, name="best%d" % b, align_bytes=64) for b in range(S // P)]
+        docs = BANK // D
+        for g in range(V // BANK):
+            for b in range(S // P):
+                acc = psum.tile([P, BANK], F32, name="acc")
+                nc.tensor.matmul_mx(
+                    out=acc[:],
+                    lhsT=h_codes[b][:].bitcast(FP8X4),
+                    lhsT_scale=h_scales[b][:],
+                    rhs=vw[g][:].bitcast(FP8X4),
+                    rhs_scale=vs[V_ROW0:P, g * BANK : (g + 1) * BANK],
+                    start=True,
+                    stop=True,
+                )
+                nc.vector.tensor_reduce(
+                    best[b][:, g * docs : (g + 1) * docs], acc[:].rearrange("p (v d) -> p v d", d=D), AXIS_X, MAX
+                )
+                if g == V // BANK - 1:
+                    nc.sync.dma_start(out=out[b * P : (b + 1) * P, :], in_=best[b][:])

@@ -23,9 +23,10 @@ PASSES = K // K_PASS
 QUADS = 4
 QUAD = 32
 ROWS = 4
-V_ROW0 = 8
+SPREAD = 8
 BANK = 512
 LIST = 16
+WARM_PASSES = 3
 
 
 def tile_picked_zlateq_gelu_p_kernel(tc, x_words, x_scales, w1, v_words, v_scales, offs, doc, out):
@@ -37,56 +38,73 @@ def tile_picked_zlateq_gelu_p_kernel(tc, x_words, x_scales, w1, v_words, v_scale
         offs_t = keep.tile([P, S // LIST], U16, name="offs_t")
         doc_t = keep.tile([P, V // LIST], U16, name="doc_t")
         xs_tab = keep.tile([P, T], U8, name="xs_tab", align_bytes=64)
-        vs_tab = keep.tile([P, G], U8, name="vs_tab", align_bytes=64)
+        vs_tab = keep.tile([P, G], U8, name="vs_tab", tag="vs_tab", align_bytes=64)
+        vs = keep.tile([P, V], U8, name="vs", align_bytes=64)
         xw_tab = [keep.tile([P, T], I32, name="xw_tab%d" % o, align_bytes=64) for o in range(PASSES)]
-        vw_tab = keep.tile([P, G], I32, name="vw_tab", align_bytes=64)
-        w_raw = [keep.tile([P, PACK, H], F32, name="w_raw%d" % o, align_bytes=64) for o in range(PASSES)]
-
-        def load_w(o):
-            nc.sync.dma_start(out=w_raw[o][:], in_=w1[o * K_PASS : (o + 1) * K_PASS, :].rearrange("(p j) c -> p j c", j=PACK))
+        w_raw = [keep.tile([P, PACK, H], F32, name="w_raw%d" % o, tag="w_raw%d" % o, align_bytes=64) for o in range(PASSES)]
+        w_rows = [w1[o * K_PASS : (o + 1) * K_PASS, :].rearrange("(p j) c -> p j c", j=PACK) for o in range(PASSES)]
 
         def load_words(tab, words):
             nc.sync.dma_start(out=tab[:], in_=words.rearrange("p n t -> p (n t)").bitcast(I32))
 
-        nc.vector.memset(xs_tab[:].bitcast(I32), 0)
-        nc.gpsimd.memset(vs_tab[:].bitcast(I32), 0)
-        load_w(0)
+        for tab, width in ((xs_tab, T), (vs_tab, G)):
+            nc.vector.memset(tab[:, : width // 2].bitcast(I32), 0)
+            nc.gpsimd.memset(tab[:, width // 2 :].bitcast(I32), 0)
+        nc.vector.memset(vs[:].bitcast(I32), 0)
+        warm_in = keep.tile([P, 1], F32, name="warm_in")
+        warm_out = keep.tile([P, 1], F32, name="warm_out")
+        nc.gpsimd.memset(warm_in[:], 0.0)
+        nc.scalar.activation(warm_out[:], warm_in[:], GELU)
+        nc.sync.dma_start(doc_t[:], doc)
+        nc.sync.dma_start(offs_t[:], offs)
+        for j in range(0, PACK, 2):
+            nc.sync.dma_start(out=w_raw[0][:, j : j + 2, :], in_=w_rows[0][:, j : j + 2, :])
         for q in range(QUADS):
             nc.sync.dma_start(
                 out=xs_tab[QUAD * q : QUAD * q + PASSES * ROWS, :].bitcast(I32),
                 in_=x_scales[:, ROWS * q : ROWS * (q + 1), :].bitcast(I32),
             )
-        nc.sync.dma_start(offs_t[:], offs)
-        nc.sync.dma_start(doc_t[:], doc)
-        for q in range(QUADS):
-            nc.gpsimd.dma_start(
-                out=vs_tab[QUAD * q + V_ROW0 : QUAD * q + V_ROW0 + ROWS, :].bitcast(I32),
-                in_=v_scales[0, ROWS * q : ROWS * (q + 1), :].bitcast(I32),
-            )
-        load_w(1)
+        nc.sync.dma_start(out=vs_tab[0:P:SPREAD, :].bitcast(I32), in_=v_scales[0].bitcast(I32))
+        nc.sync.dma_start(out=w_raw[1][:], in_=w_rows[1])
         load_words(xw_tab[0], x_words[0])
         load_words(xw_tab[1], x_words[1])
-        load_words(vw_tab, v_words[0])
 
         xs = keep.tile([P, S], U8, name="xs", align_bytes=64)
-        vs = keep.tile([P, V], U8, name="vs", align_bytes=64)
         nc.vector.tensor_copy(xs[:], xs_tab[:].indirect(offs_t[:]))
-        nc.vector.tensor_copy(vs[:], vs_tab[:].indirect(doc_t[:]))
+        vs_spread = keep.tile([P, V], U8, name="vs_spread", align_bytes=64)
+        nc.vector.tensor_copy(vs_spread[:], vs_tab[:].indirect(doc_t[:]))
+        for q in range(QUADS):
+            nc.sync.dma_start(
+                out=vs[QUAD * q : QUAD * q + ROWS, :].bitcast(I32),
+                in_=vs_spread[QUAD * q : QUAD * (q + 1) : SPREAD, :].bitcast(I32),
+            )
 
         w_codes, w_scales = [], []
         for o in range(PASSES):
             grouped = keep.tile([P, H * PACK], BF16, name="w_grouped%d" % o, align_bytes=64)
             dst = grouped[:].rearrange("p (t m j) -> p m j t", t=PACK, j=PACK)
             src = w_raw[o][:].rearrange("p j (m t) -> p m j t", t=PACK)
-            if o == 0:
-                nc.scalar.copy(dst, src)
-            else:
-                nc.vector.tensor_copy(dst, src)
+            nc.scalar.copy(dst, src)
             codes = keep.tile([P, H], U32, name="w_codes%d" % o, align_bytes=64)
-            scales = keep.tile([P, H], U8, name="w_scales%d" % o, align_bytes=64)
+            scales = keep.tile([P, H], U8, name="w_scales%d" % o, tag="vs_tab" if o == 0 else "w_scales1", align_bytes=64)
             nc.vector.quantize_mx(out=codes[:].bitcast(FP8X4), scales=scales[:], in_=grouped[:])
             w_codes.append(codes)
             w_scales.append(scales)
+
+        for n in range(WARM_PASSES):
+            acc = psum.tile([P, BANK], F32, name="acc")
+            nc.tensor.matmul_mx(
+                out=acc[:],
+                lhsT=w_codes[0][:, :P].bitcast(FP8X4),
+                lhsT_scale=w_scales[0][:, :P],
+                rhs=w_codes[1][:].bitcast(FP8X4),
+                rhs_scale=w_scales[1][:],
+                start=True,
+                stop=True,
+            )
+
+        vw_tab = keep.tile([P, G], I32, name="vw_tab", tag="w_raw0", align_bytes=64)
+        load_words(vw_tab, v_words[0])
 
         xw = [keep.tile([P, S], U32, name="xw%d" % o, align_bytes=64) for o in range(PASSES)]
         nc.vector.tensor_copy(xw[0][:], xw_tab[0][:].bitcast(U32).indirect(offs_t[:]))
@@ -97,7 +115,9 @@ def tile_picked_zlateq_gelu_p_kernel(tc, x_words, x_scales, w1, v_words, v_scale
                 xw_tab[1][:].bitcast(U32).indirect(offs_t[:, a * half // LIST : (a + 1) * half // LIST]),
             )
 
-        h_codes, h_scales = [], []
+        h_bf = keep.tile([P, S * PACK], BF16, name="h_bf", align_bytes=64)
+        h_scales = keep.tile([P, S], U8, name="h_scales", align_bytes=64)
+        h_codes = keep.tile([P, S], U32, name="h_codes", align_bytes=64)
         for b in range(S // P):
             tok = slice(b * P, (b + 1) * P)
             acc = psum.tile([P, BANK], F32, name="acc")
@@ -113,37 +133,34 @@ def tile_picked_zlateq_gelu_p_kernel(tc, x_words, x_scales, w1, v_words, v_scale
                         start=(o == 0),
                         stop=(o == PASSES - 1),
                     )
-            h_bf = keep.tile([P, P * PACK], BF16, name="h_bf%d" % b, align_bytes=64)
+            block = h_bf[:, b * K_PASS : (b + 1) * K_PASS]
             nc.scalar.activation(
-                h_bf[:].rearrange("p (n t) -> p n t", t=PACK), acc[:].rearrange("p (t n) -> p n t", t=PACK), GELU
+                block.rearrange("p (n t) -> p n t", t=PACK), acc[:].rearrange("p (t n) -> p n t", t=PACK), GELU
             )
-            codes = keep.tile([P, P], U32, name="h_codes%d" % b, align_bytes=64)
-            scales = keep.tile([P, P], U8, name="h_scales%d" % b, align_bytes=64)
-            nc.vector.quantize_mx(out=codes[:].bitcast(FP8X4), scales=scales[:], in_=h_bf[:])
-            h_codes.append(codes)
-            h_scales.append(scales)
+            nc.vector.quantize_mx(out=h_codes[:, tok].bitcast(FP8X4), scales=h_scales[:, tok], in_=block)
 
         vw = [keep.tile([P, BANK], U32, name="vw%d" % g, align_bytes=64) for g in range(V // BANK)]
         for g in range(V // BANK):
             nc.vector.tensor_copy(
                 vw[g][:], vw_tab[:].bitcast(U32).indirect(doc_t[:, g * BANK // LIST : (g + 1) * BANK // LIST])
             )
+
         best = [keep.tile([P, R], F32, name="best%d" % b, align_bytes=64) for b in range(S // P)]
         docs = BANK // D
-        for g in range(V // BANK):
-            for b in range(S // P):
-                acc = psum.tile([P, BANK], F32, name="acc")
-                nc.tensor.matmul_mx(
-                    out=acc[:],
-                    lhsT=h_codes[b][:].bitcast(FP8X4),
-                    lhsT_scale=h_scales[b][:],
-                    rhs=vw[g][:].bitcast(FP8X4),
-                    rhs_scale=vs[V_ROW0:P, g * BANK : (g + 1) * BANK],
-                    start=True,
-                    stop=True,
-                )
-                nc.vector.tensor_reduce(
-                    best[b][:, g * docs : (g + 1) * docs], acc[:].rearrange("p (v d) -> p v d", d=D), AXIS_X, MAX
-                )
-                if g == V // BANK - 1:
-                    nc.sync.dma_start(out=out[b * P : (b + 1) * P, :], in_=best[b][:])
+        order = [(0, 0), (0, 1), (1, 0), (1, 1), (0, 2), (1, 2), (0, 3), (1, 3)]
+        for g, b in order:
+            acc = psum.tile([P, BANK], F32, name="acc")
+            nc.tensor.matmul_mx(
+                out=acc[:],
+                lhsT=h_codes[:, b * P : (b + 1) * P].bitcast(FP8X4),
+                lhsT_scale=h_scales[:, b * P : (b + 1) * P],
+                rhs=vw[g][:].bitcast(FP8X4),
+                rhs_scale=vs[:, g * BANK : (g + 1) * BANK],
+                start=True,
+                stop=True,
+            )
+            nc.vector.tensor_reduce(
+                best[b][:, g * docs : (g + 1) * docs], acc[:].rearrange("p (v d) -> p v d", d=D), AXIS_X, MAX
+            )
+            if g == V // BANK - 1:
+                nc.sync.dma_start(out=out[b * P : (b + 1) * P, :], in_=best[b][:])

@@ -24,6 +24,8 @@ QUADS = 4
 QUAD = 32
 ROWS = 4
 SPREAD = 8
+X_SPREAD = 4
+QUAD_ORDER = (0, 2, 1, 3)
 BANK = 512
 LIST = 16
 WARM_PASSES = 3
@@ -37,10 +39,11 @@ def tile_picked_zlateq_gelu_p_kernel(tc, x_words, x_scales, w1, v_words, v_scale
 
         offs_t = keep.tile([P, S // LIST], U16, name="offs_t")
         doc_t = keep.tile([P, V // LIST], U16, name="doc_t")
-        xs_tab = keep.tile([P, T], U8, name="xs_tab", align_bytes=64)
+        xs_tab = keep.tile([P, T], U8, name="xs_tab", tag="xs_tab", align_bytes=64)
         vs_tab = keep.tile([P, G], U8, name="vs_tab", tag="vs_tab", align_bytes=64)
         vs = keep.tile([P, V], U8, name="vs", align_bytes=64)
-        xw_tab = [keep.tile([P, T], I32, name="xw_tab%d" % o, align_bytes=64) for o in range(PASSES)]
+        xs = keep.tile([P, S], U8, name="xs", align_bytes=64)
+        xw_tab = [keep.tile([P, T], I32, name="xw_tab0", align_bytes=64)]
         w_raw = [keep.tile([P, PACK, H], F32, name="w_raw%d" % o, tag="w_raw%d" % o, align_bytes=64) for o in range(PASSES)]
         w_rows = [w1[o * K_PASS : (o + 1) * K_PASS, :].rearrange("(p j) c -> p j c", j=PACK) for o in range(PASSES)]
 
@@ -50,6 +53,7 @@ def tile_picked_zlateq_gelu_p_kernel(tc, x_words, x_scales, w1, v_words, v_scale
         for tab, width in ((xs_tab, T), (vs_tab, G)):
             nc.vector.memset(tab[:, : width // 2].bitcast(I32), 0)
             nc.gpsimd.memset(tab[:, width // 2 :].bitcast(I32), 0)
+        nc.vector.memset(xs[:].bitcast(I32), 0)
         nc.vector.memset(vs[:].bitcast(I32), 0)
         warm_in = keep.tile([P, 1], F32, name="warm_in")
         warm_out = keep.tile([P, 1], F32, name="warm_out")
@@ -59,25 +63,28 @@ def tile_picked_zlateq_gelu_p_kernel(tc, x_words, x_scales, w1, v_words, v_scale
         nc.sync.dma_start(offs_t[:], offs)
         for j in range(0, PACK, 2):
             nc.sync.dma_start(out=w_raw[0][:, j : j + 2, :], in_=w_rows[0][:, j : j + 2, :])
-        for q in range(QUADS):
+        for q in QUAD_ORDER:
             nc.sync.dma_start(
-                out=xs_tab[QUAD * q : QUAD * q + PASSES * ROWS, :].bitcast(I32),
+                out=xs_tab[QUAD * q : QUAD * (q + 1) : X_SPREAD, :].bitcast(I32),
                 in_=x_scales[:, ROWS * q : ROWS * (q + 1), :].bitcast(I32),
             )
         nc.sync.dma_start(out=vs_tab[0:P:SPREAD, :].bitcast(I32), in_=v_scales[0].bitcast(I32))
         nc.sync.dma_start(out=w_raw[1][:], in_=w_rows[1])
         load_words(xw_tab[0], x_words[0])
-        load_words(xw_tab[1], x_words[1])
 
-        xs = keep.tile([P, S], U8, name="xs", align_bytes=64)
-        nc.vector.tensor_copy(xs[:], xs_tab[:].indirect(offs_t[:]))
+        xs_spread = keep.tile([P, S], U8, name="xs_spread", align_bytes=64)
+        nc.vector.tensor_copy(xs_spread[:], xs_tab[:].indirect(offs_t[:]))
+        for q in QUAD_ORDER:
+            nc.sync.dma_start(
+                out=xs[QUAD * q : QUAD * q + PASSES * ROWS, :].bitcast(I32),
+                in_=xs_spread[QUAD * q : QUAD * (q + 1) : X_SPREAD, :].bitcast(I32),
+            )
+        xw_tab.append(keep.tile([P, T], I32, name="xw_tab1", tag="xs_tab", align_bytes=64))
+        load_words(xw_tab[1], x_words[1])
         vs_spread = keep.tile([P, V], U8, name="vs_spread", align_bytes=64)
         nc.vector.tensor_copy(vs_spread[:], vs_tab[:].indirect(doc_t[:]))
-        for q in range(QUADS):
-            nc.sync.dma_start(
-                out=vs[QUAD * q : QUAD * q + ROWS, :].bitcast(I32),
-                in_=vs_spread[QUAD * q : QUAD * (q + 1) : SPREAD, :].bitcast(I32),
-            )
+        for r in range(ROWS):
+            nc.sync.dma_start(out=vs[r:P:QUAD, :].bitcast(I32), in_=vs_spread[SPREAD * r : P : QUAD, :].bitcast(I32))
 
         w_codes, w_scales = [], []
         for o in range(PASSES):

@@ -24,8 +24,7 @@ QUADS = 4
 QUAD = 32
 ROWS = 4
 SPREAD = 8
-X_SPREAD = 4
-QUAD_ORDER = (0, 2, 1, 3)
+V_PLANE = 8
 BANK = 512
 LIST = 16
 WARM_PASSES = 3
@@ -39,10 +38,10 @@ def tile_picked_zlateq_gelu_p_kernel(tc, x_words, x_scales, w1, v_words, v_scale
 
         offs_t = keep.tile([P, S // LIST], U16, name="offs_t")
         doc_t = keep.tile([P, V // LIST], U16, name="doc_t")
-        xs_tab = keep.tile([P, T], U8, name="xs_tab", tag="xs_tab", align_bytes=64)
+        xs_tab = keep.tile([P, PASSES * T], U8, name="xs_tab", tag="xs_tab", align_bytes=64)
         vs_tab = keep.tile([P, G], U8, name="vs_tab", tag="vs_tab", align_bytes=64)
         vs = keep.tile([P, V], U8, name="vs", align_bytes=64)
-        xs = keep.tile([P, S], U8, name="xs", align_bytes=64)
+        xs = keep.tile([P, PASSES * S], U8, name="xs", align_bytes=64)
         xw_tab = [keep.tile([P, T], I32, name="xw_tab0", align_bytes=64)]
         w_raw = [keep.tile([P, PACK, H], F32, name="w_raw%d" % o, tag="w_raw%d" % o, align_bytes=64) for o in range(PASSES)]
         w_rows = [w1[o * K_PASS : (o + 1) * K_PASS, :].rearrange("(p j) c -> p j c", j=PACK) for o in range(PASSES)]
@@ -50,7 +49,7 @@ def tile_picked_zlateq_gelu_p_kernel(tc, x_words, x_scales, w1, v_words, v_scale
         def load_words(tab, words):
             nc.sync.dma_start(out=tab[:], in_=words.rearrange("p n t -> p (n t)").bitcast(I32))
 
-        for tab, width in ((xs_tab, T), (vs_tab, G)):
+        for tab, width in ((xs_tab, PASSES * T), (vs_tab, G)):
             nc.vector.memset(tab[:, : width // 2].bitcast(I32), 0)
             nc.gpsimd.memset(tab[:, width // 2 :].bitcast(I32), 0)
         nc.vector.memset(xs[:].bitcast(I32), 0)
@@ -59,32 +58,28 @@ def tile_picked_zlateq_gelu_p_kernel(tc, x_words, x_scales, w1, v_words, v_scale
         warm_out = keep.tile([P, 1], F32, name="warm_out")
         nc.gpsimd.memset(warm_in[:], 0.0)
         nc.scalar.activation(warm_out[:], warm_in[:], GELU)
-        nc.sync.dma_start(doc_t[:], doc)
+        nc.sync.dma_start(out=w_raw[0][:], in_=w_rows[0])
         nc.sync.dma_start(offs_t[:], offs)
-        for j in range(0, PACK, 2):
-            nc.sync.dma_start(out=w_raw[0][:, j : j + 2, :], in_=w_rows[0][:, j : j + 2, :])
-        for q in QUAD_ORDER:
-            nc.sync.dma_start(
-                out=xs_tab[QUAD * q : QUAD * (q + 1) : X_SPREAD, :].bitcast(I32),
-                in_=x_scales[:, ROWS * q : ROWS * (q + 1), :].bitcast(I32),
-            )
+        nc.sync.dma_start(doc_t[:], doc)
+        nc.sync.dma_start(
+            out=xs_tab[0:P:SPREAD, :].bitcast(I32).rearrange("r (o c) -> r o c", o=PASSES),
+            in_=x_scales.bitcast(I32).rearrange("o r c -> r o c"),
+        )
         nc.sync.dma_start(out=vs_tab[0:P:SPREAD, :].bitcast(I32), in_=v_scales[0].bitcast(I32))
         nc.sync.dma_start(out=w_raw[1][:], in_=w_rows[1])
         load_words(xw_tab[0], x_words[0])
 
-        xs_spread = keep.tile([P, S], U8, name="xs_spread", align_bytes=64)
-        nc.vector.tensor_copy(xs_spread[:], xs_tab[:].indirect(offs_t[:]))
-        for q in QUAD_ORDER:
-            nc.sync.dma_start(
-                out=xs[QUAD * q : QUAD * q + PASSES * ROWS, :].bitcast(I32),
-                in_=xs_spread[QUAD * q : QUAD * (q + 1) : X_SPREAD, :].bitcast(I32),
-            )
+        xs_spread = keep.tile([P, PASSES * S], U8, name="xs_spread", align_bytes=64)
+        for o in range(PASSES):
+            nc.vector.tensor_copy(xs_spread[:, o * S : (o + 1) * S], xs_tab[:, o * T : (o + 1) * T].indirect(offs_t[:]))
+        for r in range(ROWS):
+            nc.sync.dma_start(out=xs[r:P:QUAD, :].bitcast(I32), in_=xs_spread[SPREAD * r : P : QUAD, :].bitcast(I32))
         xw_tab.append(keep.tile([P, T], I32, name="xw_tab1", tag="xs_tab", align_bytes=64))
         load_words(xw_tab[1], x_words[1])
         vs_spread = keep.tile([P, V], U8, name="vs_spread", align_bytes=64)
         nc.vector.tensor_copy(vs_spread[:], vs_tab[:].indirect(doc_t[:]))
         for r in range(ROWS):
-            nc.sync.dma_start(out=vs[r:P:QUAD, :].bitcast(I32), in_=vs_spread[SPREAD * r : P : QUAD, :].bitcast(I32))
+            nc.sync.dma_start(out=vs[V_PLANE + r : P : QUAD, :].bitcast(I32), in_=vs_spread[SPREAD * r : P : QUAD, :].bitcast(I32))
 
         w_codes, w_scales = [], []
         for o in range(PASSES):
@@ -136,7 +131,7 @@ def tile_picked_zlateq_gelu_p_kernel(tc, x_words, x_scales, w1, v_words, v_scale
                         lhsT=w_codes[o][:, ch].bitcast(FP8X4),
                         lhsT_scale=w_scales[o][:, ch],
                         rhs=xw[o][:, tok].bitcast(FP8X4),
-                        rhs_scale=xs[ROWS * o : P, tok],
+                        rhs_scale=xs[:, o * S + b * P : o * S + (b + 1) * P],
                         start=(o == 0),
                         stop=(o == PASSES - 1),
                     )
@@ -162,7 +157,7 @@ def tile_picked_zlateq_gelu_p_kernel(tc, x_words, x_scales, w1, v_words, v_scale
                 lhsT=h_codes[:, b * P : (b + 1) * P].bitcast(FP8X4),
                 lhsT_scale=h_scales[:, b * P : (b + 1) * P],
                 rhs=vw[g][:].bitcast(FP8X4),
-                rhs_scale=vs[:, g * BANK : (g + 1) * BANK],
+                rhs_scale=vs[V_PLANE:P, g * BANK : (g + 1) * BANK],
                 start=True,
                 stop=True,
             )

@@ -27,7 +27,7 @@ SPREAD = 8
 V_PLANE = 8
 BANK = 512
 LIST = 16
-WARM_PASSES = 3
+WARM_PASSES = 4
 
 
 def tile_picked_zlateq_gelu_p_kernel(tc, x_words, x_scales, w1, v_words, v_scales, offs, doc, out):
@@ -49,22 +49,22 @@ def tile_picked_zlateq_gelu_p_kernel(tc, x_words, x_scales, w1, v_words, v_scale
         def load_words(tab, words):
             nc.sync.dma_start(out=tab[:], in_=words.rearrange("p n t -> p (n t)").bitcast(I32))
 
-        for tab, width in ((xs_tab, PASSES * T), (vs_tab, G)):
-            nc.vector.memset(tab[:, : width // 2].bitcast(I32), 0)
-            nc.gpsimd.memset(tab[:, width // 2 :].bitcast(I32), 0)
-        nc.vector.memset(xs[:].bitcast(I32), 0)
-        nc.vector.memset(vs[:].bitcast(I32), 0)
+        nc.vector.memset(xs_tab[:, :T].bitcast(I32), 0)
+        nc.gpsimd.memset(xs_tab[:, T:].bitcast(I32), 0)
+        for tile in (vs_tab, xs, vs):
+            nc.vector.memset(tile[:].bitcast(I32), 0)
         warm_in = keep.tile([P, 1], F32, name="warm_in")
         warm_out = keep.tile([P, 1], F32, name="warm_out")
         nc.gpsimd.memset(warm_in[:], 0.0)
         nc.scalar.activation(warm_out[:], warm_in[:], GELU)
-        nc.sync.dma_start(out=w_raw[0][:], in_=w_rows[0])
+        nc.sync.dma_start(out=w_raw[0][:, :2, :], in_=w_rows[0][:, :2, :])
         nc.sync.dma_start(offs_t[:], offs)
         nc.sync.dma_start(doc_t[:], doc)
         nc.sync.dma_start(
             out=xs_tab[0:P:SPREAD, :].bitcast(I32).rearrange("r (o c) -> r o c", o=PASSES),
             in_=x_scales.bitcast(I32).rearrange("o r c -> r o c"),
         )
+        nc.sync.dma_start(out=w_raw[0][:, 2:, :], in_=w_rows[0][:, 2:, :])
         nc.sync.dma_start(out=vs_tab[0:P:SPREAD, :].bitcast(I32), in_=v_scales[0].bitcast(I32))
         nc.sync.dma_start(out=w_raw[1][:], in_=w_rows[1])
         load_words(xw_tab[0], x_words[0])
@@ -78,8 +78,6 @@ def tile_picked_zlateq_gelu_p_kernel(tc, x_words, x_scales, w1, v_words, v_scale
         load_words(xw_tab[1], x_words[1])
         vs_spread = keep.tile([P, V], U8, name="vs_spread", align_bytes=64)
         nc.vector.tensor_copy(vs_spread[:], vs_tab[:].indirect(doc_t[:]))
-        for r in range(ROWS):
-            nc.sync.dma_start(out=vs[V_PLANE + r : P : QUAD, :].bitcast(I32), in_=vs_spread[SPREAD * r : P : QUAD, :].bitcast(I32))
 
         w_codes, w_scales = [], []
         for o in range(PASSES):
@@ -99,14 +97,16 @@ def tile_picked_zlateq_gelu_p_kernel(tc, x_words, x_scales, w1, v_words, v_scale
                 out=acc[:],
                 lhsT=w_codes[0][:, :P].bitcast(FP8X4),
                 lhsT_scale=w_scales[0][:, :P],
-                rhs=w_codes[1][:].bitcast(FP8X4),
-                rhs_scale=w_scales[1][:],
+                rhs=w_codes[0][:].bitcast(FP8X4),
+                rhs_scale=w_scales[0][:],
                 start=True,
                 stop=True,
             )
 
         vw_tab = keep.tile([P, G], I32, name="vw_tab", tag="w_raw0", align_bytes=64)
         load_words(vw_tab, v_words[0])
+        for r in range(ROWS):
+            nc.sync.dma_start(out=vs[V_PLANE + r : P : QUAD, :].bitcast(I32), in_=vs_spread[SPREAD * r : P : QUAD, :].bitcast(I32))
 
         xw = [keep.tile([P, S], U32, name="xw%d" % o, align_bytes=64) for o in range(PASSES)]
         nc.vector.tensor_copy(xw[0][:], xw_tab[0][:].bitcast(U32).indirect(offs_t[:]))

@@ -104,9 +104,11 @@ def tile_picked_zlateq_gelu_p_kernel(tc, x_words, x_scales, w1, v_words, v_scale
             )
 
         vw_tab = keep.tile([P, G], I32, name="vw_tab", tag="w_raw0", align_bytes=64)
-        load_words(vw_tab, v_words[0])
+        v_rows = v_words[0].rearrange("p n t -> p (n t)").bitcast(I32)
+        nc.sync.dma_start(out=vw_tab[:, : G // 2], in_=v_rows[:, : G // 2])
         for r in range(ROWS):
             nc.sync.dma_start(out=vs[V_PLANE + r : P : QUAD, :].bitcast(I32), in_=vs_spread[SPREAD * r : P : QUAD, :].bitcast(I32))
+        nc.sync.dma_start(out=vw_tab[:, G // 2 :], in_=v_rows[:, G // 2 :])
 
         xw = [keep.tile([P, S], U32, name="xw%d" % o, align_bytes=64) for o in range(PASSES)]
         nc.vector.tensor_copy(xw[0][:], xw_tab[0][:].bitcast(U32).indirect(offs_t[:]))

@@ -151,7 +151,7 @@ def tile_picked_zlateq_gelu_p_kernel(tc, x_words, x_scales, w1, v_words, v_scale
 
         best = [keep.tile([P, R], F32, name="best%d" % b, align_bytes=64) for b in range(S // P)]
         docs = BANK // D
-        order = [(0, 0), (0, 1), (1, 0), (1, 1), (0, 2), (1, 2), (0, 3), (1, 3)]
+        order = [(g, b) for g in range(V // BANK) for b in range(S // P)]
         for g, b in order:
             acc = psum.tile([P, BANK], F32, name="acc")
             nc.tensor.matmul_mx(

@@ -23,7 +23,9 @@ PASSES = K // K_PASS
 QUADS = 4
 QUAD = 32
 ROWS = 4
-SPREAD = 8
+SPREAD = 7
+FIRST = 17
+TABLE_ROWS = slice(FIRST, FIRST + 15 * SPREAD + 1, SPREAD)
 V_PLANE = 8
 BANK = 512
 LIST = 16
@@ -61,11 +63,11 @@ def tile_picked_zlateq_gelu_p_kernel(tc, x_words, x_scales, w1, v_words, v_scale
         nc.sync.dma_start(offs_t[:], offs)
         nc.sync.dma_start(doc_t[:], doc)
         nc.sync.dma_start(
-            out=xs_tab[0:P:SPREAD, :].bitcast(I32).rearrange("r (o c) -> r o c", o=PASSES),
+            out=xs_tab[TABLE_ROWS, :].bitcast(I32).rearrange("r (o c) -> r o c", o=PASSES),
             in_=x_scales.bitcast(I32).rearrange("o r c -> r o c"),
         )
         nc.sync.dma_start(out=w_raw[0][:, 2:, :], in_=w_rows[0][:, 2:, :])
-        nc.sync.dma_start(out=vs_tab[0:P:SPREAD, :].bitcast(I32), in_=v_scales[0].bitcast(I32))
+        nc.sync.dma_start(out=vs_tab[TABLE_ROWS, :].bitcast(I32), in_=v_scales[0].bitcast(I32))
         nc.sync.dma_start(out=w_raw[1][:], in_=w_rows[1])
         load_words(xw_tab[0], x_words[0])
 
@@ -73,7 +75,7 @@ def tile_picked_zlateq_gelu_p_kernel(tc, x_words, x_scales, w1, v_words, v_scale
         for o in range(PASSES):
             nc.vector.tensor_copy(xs_spread[:, o * S : (o + 1) * S], xs_tab[:, o * T : (o + 1) * T].indirect(offs_t[:]))
         for r in range(ROWS):
-            nc.sync.dma_start(out=xs[r:P:QUAD, :].bitcast(I32), in_=xs_spread[SPREAD * r : P : QUAD, :].bitcast(I32))
+            nc.sync.dma_start(out=xs[r:P:QUAD, :].bitcast(I32), in_=xs_spread[FIRST + SPREAD * r : FIRST + 15 * SPREAD + 1 : ROWS * SPREAD, :].bitcast(I32))
         xw_tab.append(keep.tile([P, T], I32, name="xw_tab1", tag="xs_tab", align_bytes=64))
         load_words(xw_tab[1], x_words[1])
         vs_spread = keep.tile([P, V], U8, name="vs_spread", align_bytes=64)
@@ -107,7 +109,7 @@ def tile_picked_zlateq_gelu_p_kernel(tc, x_words, x_scales, w1, v_words, v_scale
         v_rows = v_words[0].rearrange("p n t -> p (n t)").bitcast(I32)
         nc.sync.dma_start(out=vw_tab[:, : G // 2], in_=v_rows[:, : G // 2])
         for r in range(ROWS):
-            nc.sync.dma_start(out=vs[V_PLANE + r : P : QUAD, :].bitcast(I32), in_=vs_spread[SPREAD * r : P : QUAD, :].bitcast(I32))
+            nc.sync.dma_start(out=vs[V_PLANE + r : P : QUAD, :].bitcast(I32), in_=vs_spread[FIRST + SPREAD * r : FIRST + 15 * SPREAD + 1 : ROWS * SPREAD, :].bitcast(I32))
         nc.sync.dma_start(out=vw_tab[:, G // 2 :], in_=v_rows[:, G // 2 :])
 
         xw = [keep.tile([P, S], U32, name="xw%d" % o, align_bytes=64) for o in range(PASSES)]

@@ -44,7 +44,7 @@ def tile_picked_zlateq_gelu_p_kernel(tc, x_words, x_scales, w1, v_words, v_scale
         vs_tab = keep.tile([P, G], U8, name="vs_tab", tag="vs_tab", align_bytes=64)
         vs = keep.tile([P, V], U8, name="vs", align_bytes=64)
         xs = keep.tile([P, PASSES * S], U8, name="xs", align_bytes=64)
-        xw_tab = [keep.tile([P, T], I32, name="xw_tab0", align_bytes=64)]
+        xw_tab = [keep.tile([P, T], I32, name="xw_tab0", tag="xw_tab0", align_bytes=64)]
         w_raw = [keep.tile([P, PACK, H], F32, name="w_raw%d" % o, tag="w_raw%d" % o, align_bytes=64) for o in range(PASSES)]
         w_rows = [w1[o * K_PASS : (o + 1) * K_PASS, :].rearrange("(p j) c -> p j c", j=PACK) for o in range(PASSES)]
 
@@ -81,6 +81,16 @@ def tile_picked_zlateq_gelu_p_kernel(tc, x_words, x_scales, w1, v_words, v_scale
         vs_spread = keep.tile([P, V], U8, name="vs_spread", align_bytes=64)
         nc.vector.tensor_copy(vs_spread[:], vs_tab[:].indirect(doc_t[:]))
 
+        xw = [keep.tile([P, S], U32, name="xw%d" % o, align_bytes=64) for o in range(PASSES)]
+        half = S // 2
+
+        def pick_words(o):
+            for a in range(2):
+                nc.vector.tensor_copy(
+                    xw[o][:, a * half : (a + 1) * half],
+                    xw_tab[o][:].bitcast(U32).indirect(offs_t[:, a * half // LIST : (a + 1) * half // LIST]),
+                )
+
         w_codes, w_scales = [], []
         for o in range(PASSES):
             grouped = keep.tile([P, H * PACK], BF16, name="w_grouped%d" % o, align_bytes=64)
@@ -88,22 +98,12 @@ def tile_picked_zlateq_gelu_p_kernel(tc, x_words, x_scales, w1, v_words, v_scale
             src = w_raw[o][:].rearrange("p j (m t) -> p m j t", t=PACK)
             nc.scalar.copy(dst, src)
             codes = keep.tile([P, H], U32, name="w_codes%d" % o, align_bytes=64)
-            scales = keep.tile([P, H], U8, name="w_scales%d" % o, tag="vs_tab" if o == 0 else "w_scales1", align_bytes=64)
+            scales = keep.tile([P, H], U8, name="w_scales%d" % o, tag="vs_tab" if o == 0 else "xw_tab0", align_bytes=64)
             nc.vector.quantize_mx(out=codes[:].bitcast(FP8X4), scales=scales[:], in_=grouped[:])
             w_codes.append(codes)
             w_scales.append(scales)
-
-        for n in range(WARM_PASSES):
-            acc = psum.tile([P, BANK], F32, name="acc")
-            nc.tensor.matmul_mx(
-                out=acc[:],
-                lhsT=w_codes[0][:, :P].bitcast(FP8X4),
-                lhsT_scale=w_scales[0][:, :P],
-                rhs=w_codes[0][:].bitcast(FP8X4),
-                rhs_scale=w_scales[0][:],
-                start=True,
-                stop=True,
-            )
+            if o == 0:
+                pick_words(0)
 
         vw_tab = keep.tile([P, G], I32, name="vw_tab", tag="w_raw0", align_bytes=64)
         v_rows = v_words[0].rearrange("p n t -> p (n t)").bitcast(I32)
@@ -112,38 +112,49 @@ def tile_picked_zlateq_gelu_p_kernel(tc, x_words, x_scales, w1, v_words, v_scale
             nc.sync.dma_start(out=vs[V_PLANE + r : P : QUAD, :].bitcast(I32), in_=vs_spread[FIRST + SPREAD * r : FIRST + 15 * SPREAD + 1 : ROWS * SPREAD, :].bitcast(I32))
         nc.sync.dma_start(out=vw_tab[:, G // 2 :], in_=v_rows[:, G // 2 :])
 
-        xw = [keep.tile([P, S], U32, name="xw%d" % o, align_bytes=64) for o in range(PASSES)]
-        nc.vector.tensor_copy(xw[0][:], xw_tab[0][:].bitcast(U32).indirect(offs_t[:]))
-        half = S // 2
-        for a in range(2):
-            nc.vector.tensor_copy(
-                xw[1][:, a * half : (a + 1) * half],
-                xw_tab[1][:].bitcast(U32).indirect(offs_t[:, a * half // LIST : (a + 1) * half // LIST]),
-            )
+        pick_words(1)
 
         h_bf = keep.tile([P, S * PACK], BF16, name="h_bf", align_bytes=64)
         h_scales = keep.tile([P, S], U8, name="h_scales", align_bytes=64)
         h_codes = keep.tile([P, S], U32, name="h_codes", align_bytes=64)
-        for b in range(S // P):
-            tok = slice(b * P, (b + 1) * P)
-            acc = psum.tile([P, BANK], F32, name="acc")
+        accs = [psum.tile([P, BANK], F32, name="acc", bufs=7) for b in range(S // P)]
+
+        def project(o, b):
             for t in range(PACK):
                 ch = slice(t * P, (t + 1) * P)
-                for o in range(PASSES):
-                    nc.tensor.matmul_mx(
-                        out=acc[:, ch],
-                        lhsT=w_codes[o][:, ch].bitcast(FP8X4),
-                        lhsT_scale=w_scales[o][:, ch],
-                        rhs=xw[o][:, tok].bitcast(FP8X4),
-                        rhs_scale=xs[:, o * S + b * P : o * S + (b + 1) * P],
-                        start=(o == 0),
-                        stop=(o == PASSES - 1),
-                    )
+                nc.tensor.matmul_mx(
+                    out=accs[b][:, ch],
+                    lhsT=w_codes[o][:, ch].bitcast(FP8X4),
+                    lhsT_scale=w_scales[o][:, ch],
+                    rhs=xw[o][:, b * P : (b + 1) * P].bitcast(FP8X4),
+                    rhs_scale=xs[:, o * S + b * P : o * S + (b + 1) * P],
+                    start=(o == 0 and t == 0),
+                    stop=(o == PASSES - 1 and t == PACK - 1),
+                )
+
+        for b in range(S // P):
+            project(0, b)
+        for b in range(S // P):
+            tok = slice(b * P, (b + 1) * P)
+            acc = accs[b]
+            project(1, b)
             block = h_bf[:, b * K_PASS : (b + 1) * K_PASS]
             nc.scalar.activation(
                 block.rearrange("p (n t) -> p n t", t=PACK), acc[:].rearrange("p (t n) -> p n t", t=PACK), GELU
             )
             nc.vector.quantize_mx(out=h_codes[:, tok].bitcast(FP8X4), scales=h_scales[:, tok], in_=block)
+            if b >= 2:
+                for n in range(WARM_PASSES // 2):
+                    warm = psum.tile([P, BANK], F32, name="acc", bufs=7)
+                    nc.tensor.matmul_mx(
+                        out=warm[:],
+                        lhsT=h_codes[:, tok].bitcast(FP8X4),
+                        lhsT_scale=h_scales[:, tok],
+                        rhs=w_codes[0][:].bitcast(FP8X4),
+                        rhs_scale=w_scales[0][:],
+                        start=True,
+                        stop=True,
+                    )
 
         vw = [keep.tile([P, BANK], U32, name="vw%d" % g, align_bytes=64) for g in range(V // BANK)]
         for g in range(V // BANK):
@@ -151,11 +162,21 @@ def tile_picked_zlateq_gelu_p_kernel(tc, x_words, x_scales, w1, v_words, v_scale
                 vw[g][:], vw_tab[:].bitcast(U32).indirect(doc_t[:, g * BANK // LIST : (g + 1) * BANK // LIST])
             )
 
-        best = [keep.tile([P, R], F32, name="best%d" % b, align_bytes=64) for b in range(S // P)]
+        blocks = S // P
         docs = BANK // D
-        order = [(g, b) for g in range(V // BANK) for b in range(S // P)]
-        for g, b in order:
-            acc = psum.tile([P, BANK], F32, name="acc")
+        tree = blocks - 1
+        groups = V // BANK
+        best = keep.tile([P, tree * groups, docs], F32, name="best", align_bytes=64)
+        plain = keep.tile([P, R], F32, name="plain", align_bytes=64)
+        out_rows = out.rearrange("(b p) v -> p b v", p=P)
+        fours = keep.tile([P, tree * groups, docs * 4], F32, name="fours", align_bytes=64)
+        twos = keep.tile([P, tree * groups, docs * 2], F32, name="twos", align_bytes=64)
+
+        def score(g, b):
+            if g == groups - 1 and b in (0, blocks - 1):
+                acc = psum.tile([P, BANK], F32, name="acc_end", bufs=1)
+            else:
+                acc = psum.tile([P, BANK], F32, name="acc", bufs=7)
             nc.tensor.matmul_mx(
                 out=acc[:],
                 lhsT=h_codes[:, b * P : (b + 1) * P].bitcast(FP8X4),
@@ -165,8 +186,31 @@ def tile_picked_zlateq_gelu_p_kernel(tc, x_words, x_scales, w1, v_words, v_scale
                 start=True,
                 stop=True,
             )
+            return acc
+
+        def reduce_docs(g):
             nc.vector.tensor_reduce(
-                best[b][:, g * docs : (g + 1) * docs], acc[:].rearrange("p (v d) -> p v d", d=D), AXIS_X, MAX
+                plain[:, g * docs : (g + 1) * docs], score(g, 0)[:].rearrange("p (v d) -> p v d", d=D), AXIS_X, MAX
             )
-            if g == V // BANK - 1:
-                nc.sync.dma_start(out=out[b * P : (b + 1) * P, :], in_=best[b][:])
+
+        def to_four(g, b):
+            tokens = score(g, b)[:].rearrange("p (v d) -> p d v", d=D)
+            upper = keep.tile([P, 4, docs], F32, name="upper%d%d" % (g, b), align_bytes=64)
+            nc.scalar.copy(upper[:], tokens[:, 4:, :])
+            dst = fours[:, (b - 1) * groups + g, :]
+            nc.vector.tensor_tensor(dst.rearrange("p (d v) -> p d v", d=4), tokens[:, :4, :], upper[:], MAX)
+
+        reduce_docs(0)
+        for g in range(groups):
+            for b in range(1, blocks):
+                to_four(g, b)
+        runs = [(1, blocks - 1), (blocks - 1, blocks)]
+        for lo, hi in runs:
+            run = slice((lo - 1) * groups, (hi - 1) * groups)
+            nc.vector.tensor_tensor(twos[:, run, :], fours[:, run, : docs * 2], fours[:, run, docs * 2 :], MAX)
+        for lo, hi in runs:
+            run = slice((lo - 1) * groups, (hi - 1) * groups)
+            nc.vector.tensor_tensor(best[:, run, :], twos[:, run, :docs], twos[:, run, docs:], MAX)
+            nc.sync.dma_start(out=out_rows[:, lo:hi, :], in_=best[:, run, :].rearrange("p (b g) v -> p b (g v)", g=groups))
+        reduce_docs(1)
+        nc.sync.dma_start(out=out_rows[:, 0, :], in_=plain[:])

@@ -91,6 +91,19 @@ def tile_picked_zlateq_gelu_p_kernel(tc, x_words, x_scales, w1, v_words, v_scale
                     xw_tab[o][:].bitcast(U32).indirect(offs_t[:, a * half // LIST : (a + 1) * half // LIST]),
                 )
 
+        def warm_up(codes, scales):
+            for n in range(WARM_PASSES // 2):
+                warm = psum.tile([P, BANK], F32, name="acc", bufs=7)
+                nc.tensor.matmul_mx(
+                    out=warm[:],
+                    lhsT=codes.bitcast(FP8X4),
+                    lhsT_scale=scales,
+                    rhs=w_codes[0][:].bitcast(FP8X4),
+                    rhs_scale=w_scales[0][:],
+                    start=True,
+                    stop=True,
+                )
+
         w_codes, w_scales = [], []
         for o in range(PASSES):
             grouped = keep.tile([P, H * PACK], BF16, name="w_grouped%d" % o, align_bytes=64)
@@ -98,11 +111,12 @@ def tile_picked_zlateq_gelu_p_kernel(tc, x_words, x_scales, w1, v_words, v_scale
             src = w_raw[o][:].rearrange("p j (m t) -> p m j t", t=PACK)
             nc.scalar.copy(dst, src)
             codes = keep.tile([P, H], U32, name="w_codes%d" % o, align_bytes=64)
-            scales = keep.tile([P, H], U8, name="w_scales%d" % o, tag="vs_tab" if o == 0 else "xw_tab0", align_bytes=64)
+            scales = keep.tile([P, H], U8, name="w_scales%d" % o, tag="w_scales0" if o == 0 else "xw_tab0", align_bytes=64)
             nc.vector.quantize_mx(out=codes[:].bitcast(FP8X4), scales=scales[:], in_=grouped[:])
             w_codes.append(codes)
             w_scales.append(scales)
             if o == 0:
+                warm_up(codes[:, :P], scales[:, :P])
                 pick_words(0)
 
         vw_tab = keep.tile([P, G], I32, name="vw_tab", tag="w_raw0", align_bytes=64)
@@ -143,18 +157,8 @@ def tile_picked_zlateq_gelu_p_kernel(tc, x_words, x_scales, w1, v_words, v_scale
                 block.rearrange("p (n t) -> p n t", t=PACK), acc[:].rearrange("p (t n) -> p n t", t=PACK), GELU
             )
             nc.vector.quantize_mx(out=h_codes[:, tok].bitcast(FP8X4), scales=h_scales[:, tok], in_=block)
-            if b >= 2:
-                for n in range(WARM_PASSES // 2):
-                    warm = psum.tile([P, BANK], F32, name="acc", bufs=7)
-                    nc.tensor.matmul_mx(
-                        out=warm[:],
-                        lhsT=h_codes[:, tok].bitcast(FP8X4),
-                        lhsT_scale=h_scales[:, tok],
-                        rhs=w_codes[0][:].bitcast(FP8X4),
-                        rhs_scale=w_scales[0][:],
-                        start=True,
-                        stop=True,
-                    )
+            if b == 2:
+                warm_up(h_codes[:, tok], h_scales[:, tok])
 
         vw = [keep.tile([P, BANK], U32, name="vw%d" % g, align_bytes=64) for g in range(V // BANK)]
         for g in range(V // BANK):

@@ -93,7 +93,7 @@ def tile_picked_zlateq_gelu_p_kernel(tc, x_words, x_scales, w1, v_words, v_scale
 
         def warm_up(codes, scales):
             for n in range(WARM_PASSES // 2):
-                warm = psum.tile([P, BANK], F32, name="acc", bufs=7)
+                warm = psum.tile([P, BANK], F32, name="acc")
                 nc.tensor.matmul_mx(
                     out=warm[:],
                     lhsT=codes.bitcast(FP8X4),
@@ -131,7 +131,7 @@ def tile_picked_zlateq_gelu_p_kernel(tc, x_words, x_scales, w1, v_words, v_scale
         h_bf = keep.tile([P, S * PACK], BF16, name="h_bf", align_bytes=64)
         h_scales = keep.tile([P, S], U8, name="h_scales", align_bytes=64)
         h_codes = keep.tile([P, S], U32, name="h_codes", align_bytes=64)
-        accs = [psum.tile([P, BANK], F32, name="acc", bufs=7) for b in range(S // P)]
+        accs = [psum.tile([P, BANK], F32, name="acc") for b in range(S // P)]
 
         def project(o, b):
             for t in range(PACK):
@@ -166,21 +166,11 @@ def tile_picked_zlateq_gelu_p_kernel(tc, x_words, x_scales, w1, v_words, v_scale
                 vw[g][:], vw_tab[:].bitcast(U32).indirect(doc_t[:, g * BANK // LIST : (g + 1) * BANK // LIST])
             )
 
-        blocks = S // P
+        best = [keep.tile([P, R], F32, name="best%d" % b, align_bytes=64) for b in range(S // P)]
         docs = BANK // D
-        tree = blocks - 1
-        groups = V // BANK
-        best = keep.tile([P, tree * groups, docs], F32, name="best", align_bytes=64)
-        plain = keep.tile([P, R], F32, name="plain", align_bytes=64)
-        out_rows = out.rearrange("(b p) v -> p b v", p=P)
-        fours = keep.tile([P, tree * groups, docs * 4], F32, name="fours", align_bytes=64)
-        twos = keep.tile([P, tree * groups, docs * 2], F32, name="twos", align_bytes=64)
-
-        def score(g, b):
-            if g == groups - 1 and b in (0, blocks - 1):
-                acc = psum.tile([P, BANK], F32, name="acc_end", bufs=1)
-            else:
-                acc = psum.tile([P, BANK], F32, name="acc", bufs=7)
+        order = [(g, b) for g in range(V // BANK) for b in range(S // P)]
+        for g, b in order:
+            acc = psum.tile([P, BANK], F32, name="acc")
             nc.tensor.matmul_mx(
                 out=acc[:],
                 lhsT=h_codes[:, b * P : (b + 1) * P].bitcast(FP8X4),
@@ -190,31 +180,8 @@ def tile_picked_zlateq_gelu_p_kernel(tc, x_words, x_scales, w1, v_words, v_scale
                 start=True,
                 stop=True,
             )
-            return acc
-
-        def reduce_docs(g):
             nc.vector.tensor_reduce(
-                plain[:, g * docs : (g + 1) * docs], score(g, 0)[:].rearrange("p (v d) -> p v d", d=D), AXIS_X, MAX
+                best[b][:, g * docs : (g + 1) * docs], acc[:].rearrange("p (v d) -> p v d", d=D), AXIS_X, MAX
             )
-
-        def to_four(g, b):
-            tokens = score(g, b)[:].rearrange("p (v d) -> p d v", d=D)
-            upper = keep.tile([P, 4, docs], F32, name="upper%d%d" % (g, b), align_bytes=64)
-            nc.scalar.copy(upper[:], tokens[:, 4:, :])
-            dst = fours[:, (b - 1) * groups + g, :]
-            nc.vector.tensor_tensor(dst.rearrange("p (d v) -> p d v", d=4), tokens[:, :4, :], upper[:], MAX)
-
-        reduce_docs(0)
-        for g in range(groups):
-            for b in range(1, blocks):
-                to_four(g, b)
-        runs = [(1, blocks - 1), (blocks - 1, blocks)]
-        for lo, hi in runs:
-            run = slice((lo - 1) * groups, (hi - 1) * groups)
-            nc.vector.tensor_tensor(twos[:, run, :], fours[:, run, : docs * 2], fours[:, run, docs * 2 :], MAX)
-        for lo, hi in runs:
-            run = slice((lo - 1) * groups, (hi - 1) * groups)
-            nc.vector.tensor_tensor(best[:, run, :], twos[:, run, :docs], twos[:, run, docs:], MAX)
-            nc.sync.dma_start(out=out_rows[:, lo:hi, :], in_=best[:, run, :].rearrange("p (b g) v -> p b (g v)", g=groups))
-        reduce_docs(1)
-        nc.sync.dma_start(out=out_rows[:, 0, :], in_=plain[:])
+            if g == V // BANK - 1:
+                nc.sync.dma_start(out=out[b * P : (b + 1) * P, :], in_=best[b][:])

@@ -122,9 +122,9 @@ def tile_picked_zlateq_gelu_p_kernel(tc, x_words, x_scales, w1, v_words, v_scale
         vw_tab = keep.tile([P, G], I32, name="vw_tab", tag="w_raw0", align_bytes=64)
         v_rows = v_words[0].rearrange("p n t -> p (n t)").bitcast(I32)
         nc.sync.dma_start(out=vw_tab[:, : G // 2], in_=v_rows[:, : G // 2])
+        nc.sync.dma_start(out=vw_tab[:, G // 2 :], in_=v_rows[:, G // 2 :])
         for r in range(ROWS):
             nc.sync.dma_start(out=vs[V_PLANE + r : P : QUAD, :].bitcast(I32), in_=vs_spread[FIRST + SPREAD * r : FIRST + 15 * SPREAD + 1 : ROWS * SPREAD, :].bitcast(I32))
-        nc.sync.dma_start(out=vw_tab[:, G // 2 :], in_=v_rows[:, G // 2 :])
 
         pick_words(1)
 

@@ -166,10 +166,14 @@ def tile_picked_zlateq_gelu_p_kernel(tc, x_words, x_scales, w1, v_words, v_scale
                 vw[g][:], vw_tab[:].bitcast(U32).indirect(doc_t[:, g * BANK // LIST : (g + 1) * BANK // LIST])
             )
 
-        best = [keep.tile([P, R], F32, name="best%d" % b, align_bytes=64) for b in range(S // P)]
         docs = BANK // D
-        order = [(g, b) for g in range(V // BANK) for b in range(S // P)]
-        for g, b in order:
+        blocks = S // P
+        parts = [range(1, 3), range(3, 4)]
+        quads = keep.tile([P, blocks - 1, R, 4], F32, name="quads", tag="quads", align_bytes=64)
+        pairs = [keep.tile([P, len(part), R, 2], F32, name="pairs%d" % n, tag="pairs%d" % n, align_bytes=64) for n, part in enumerate(parts)]
+        best = [keep.tile([P, len(part), R], F32, name="best%d" % n, align_bytes=64) for n, part in enumerate(parts)]
+
+        def score(g, b):
             acc = psum.tile([P, BANK], F32, name="acc")
             nc.tensor.matmul_mx(
                 out=acc[:],
@@ -180,8 +184,29 @@ def tile_picked_zlateq_gelu_p_kernel(tc, x_words, x_scales, w1, v_words, v_scale
                 start=True,
                 stop=True,
             )
-            nc.vector.tensor_reduce(
-                best[b][:, g * docs : (g + 1) * docs], acc[:].rearrange("p (v d) -> p v d", d=D), AXIS_X, MAX
+            return acc[:].rearrange("p (v d) -> p v d", d=D)
+
+        def reduce_whole(g, b, tag):
+            whole = keep.tile([P, docs], F32, name="whole%d" % g, tag=tag, align_bytes=64)
+            nc.vector.tensor_reduce(whole[:], score(g, b), AXIS_X, MAX)
+            nc.sync.dma_start(out=out[b * P : (b + 1) * P, g * docs : (g + 1) * docs], in_=whole[:])
+
+        def reduce_half(g, b):
+            scores = score(g, b)
+            upper = keep.tile([P, docs, 4], F32, name="upper%d_%d" % (g, b), align_bytes=64)
+            nc.scalar.copy(upper[:], scores[:, :, 4:])
+            nc.vector.tensor_tensor(quads[:, b - 1, g * docs : (g + 1) * docs, :], scores[:, :, :4], upper[:], MAX)
+
+        reduce_whole(0, 0, "whole0")
+        for g in range(V // BANK):
+            for b in range(1, blocks):
+                reduce_half(g, b)
+        for n, part in enumerate(parts):
+            mine = quads[:, part.start - 1 : part.stop - 1, :, :]
+            nc.vector.tensor_tensor(pairs[n][:], mine[:, :, :, :2], mine[:, :, :, 2:], MAX)
+        for n, part in enumerate(parts):
+            nc.vector.tensor_tensor(best[n][:], pairs[n][:, :, :, 0], pairs[n][:, :, :, 1], MAX)
+            nc.sync.dma_start(
+                out=out[part.start * P : part.stop * P, :].rearrange("(b p) r -> p b r", p=P), in_=best[n][:]
             )
-            if g == V // BANK - 1:
-                nc.sync.dma_start(out=out[b * P : (b + 1) * P, :], in_=best[b][:])
+        reduce_whole(1, 0, "quads")

@@ -57,7 +57,7 @@ def tile_picked_zlateq_gelu_p_kernel(tc, x_words, x_scales, w1, v_words, v_scale
             nc.vector.memset(tile[:].bitcast(I32), 0)
         warm_in = keep.tile([P, 1], F32, name="warm_in")
         warm_out = keep.tile([P, 1], F32, name="warm_out")
-        nc.gpsimd.memset(warm_in[:], 0.0)
+        nc.vector.memset(warm_in[:], 0.0)
         nc.scalar.activation(warm_out[:], warm_in[:], GELU)
         nc.sync.dma_start(out=w_raw[0][:, :2, :], in_=w_rows[0][:, :2, :])
         nc.sync.dma_start(offs_t[:], offs)
@@ -198,12 +198,16 @@ def tile_picked_zlateq_gelu_p_kernel(tc, x_words, x_scales, w1, v_words, v_scale
             nc.vector.tensor_tensor(quads[:, b - 1, g * docs : (g + 1) * docs, :], scores[:, :, :4], upper[:], MAX)
 
         reduce_whole(0, 0, "whole0")
+
+        def halve(n, cols):
+            mine = quads[:, parts[n].start - 1 : parts[n].stop - 1, cols, :]
+            nc.vector.tensor_tensor(pairs[n][:, :, cols, :], mine[:, :, :, :2], mine[:, :, :, 2:], MAX)
+
         for g in range(V // BANK):
             for b in range(1, blocks):
                 reduce_half(g, b)
-        for n, part in enumerate(parts):
-            mine = quads[:, part.start - 1 : part.stop - 1, :, :]
-            nc.vector.tensor_tensor(pairs[n][:], mine[:, :, :, :2], mine[:, :, :, 2:], MAX)
+            halve(0, slice(g * docs, (g + 1) * docs))
+        halve(1, slice(0, R))
         for n, part in enumerate(parts):
             nc.vector.tensor_tensor(best[n][:], pairs[n][:, :, :, 0], pairs[n][:, :, :, 1], MAX)
             nc.sync.dma_start(

@@ -120,9 +120,7 @@ def tile_picked_zlateq_gelu_p_kernel(tc, x_words, x_scales, w1, v_words, v_scale
                 pick_words(0)
 
         vw_tab = keep.tile([P, G], I32, name="vw_tab", tag="w_raw0", align_bytes=64)
-        v_rows = v_words[0].rearrange("p n t -> p (n t)").bitcast(I32)
-        nc.sync.dma_start(out=vw_tab[:, : G // 2], in_=v_rows[:, : G // 2])
-        nc.sync.dma_start(out=vw_tab[:, G // 2 :], in_=v_rows[:, G // 2 :])
+        load_words(vw_tab, v_words[0])
         for r in range(ROWS):
             nc.sync.dma_start(out=vs[V_PLANE + r : P : QUAD, :].bitcast(I32), in_=vs_spread[FIRST + SPREAD * r : FIRST + 15 * SPREAD + 1 : ROWS * SPREAD, :].bitcast(I32))
 
@@ -210,7 +208,6 @@ def tile_picked_zlateq_gelu_p_kernel(tc, x_words, x_scales, w1, v_words, v_scale
         halve(1, slice(0, R))
         for n, part in enumerate(parts):
             nc.vector.tensor_tensor(best[n][:], pairs[n][:, :, :, 0], pairs[n][:, :, :, 1], MAX)
-            nc.sync.dma_start(
-                out=out[part.start * P : part.stop * P, :].rearrange("(b p) r -> p b r", p=P), in_=best[n][:]
-            )
+            for b in part:
+                nc.sync.dma_start(out=out[b * P : (b + 1) * P, :], in_=best[n][:, b - part.start, :])
         reduce_whole(1, 0, "quads")

@@ -29,14 +29,14 @@ TABLE_ROWS = slice(FIRST, FIRST + 15 * SPREAD + 1, SPREAD)
 V_PLANE = 8
 BANK = 512
 LIST = 16
-WARM_PASSES = 4
+BLOCKS = S // P
 
 
 def tile_picked_zlateq_gelu_p_kernel(tc, x_words, x_scales, w1, v_words, v_scales, offs, doc, out):
     nc = tc.nc
     with ExitStack() as ctx:
         keep = ctx.enter_context(tc.tile_pool(name="keep", bufs=1))
-        psum = ctx.enter_context(tc.psum_pool(name="psum", bufs=8))
+        psum = ctx.enter_context(tc.psum_pool(name="psum", bufs=1))
 
         offs_t = keep.tile([P, S // LIST], U16, name="offs_t")
         doc_t = keep.tile([P, V // LIST], U16, name="doc_t")
@@ -82,27 +82,13 @@ def tile_picked_zlateq_gelu_p_kernel(tc, x_words, x_scales, w1, v_words, v_scale
         nc.vector.tensor_copy(vs_spread[:], vs_tab[:].indirect(doc_t[:]))
 
         xw = [keep.tile([P, S], U32, name="xw%d" % o, align_bytes=64) for o in range(PASSES)]
-        half = S // 2
 
-        def pick_words(o):
-            for a in range(2):
-                nc.vector.tensor_copy(
-                    xw[o][:, a * half : (a + 1) * half],
-                    xw_tab[o][:].bitcast(U32).indirect(offs_t[:, a * half // LIST : (a + 1) * half // LIST]),
-                )
+        def pick(dst, tab, lst, lo, hi):
+            nc.vector.tensor_copy(dst, tab[:].bitcast(U32).indirect(lst[:, lo // LIST : hi // LIST]))
 
-        def warm_up(codes, scales):
-            for n in range(WARM_PASSES // 2):
-                warm = psum.tile([P, BANK], F32, name="acc")
-                nc.tensor.matmul_mx(
-                    out=warm[:],
-                    lhsT=codes.bitcast(FP8X4),
-                    lhsT_scale=scales,
-                    rhs=w_codes[0][:].bitcast(FP8X4),
-                    rhs_scale=w_scales[0][:],
-                    start=True,
-                    stop=True,
-                )
+        def pick_words(o, cuts):
+            for lo, hi in zip(cuts, cuts[1:]):
+                pick(xw[o][:, lo:hi], xw_tab[o], offs_t, lo, hi)
 
         w_codes, w_scales = [], []
         for o in range(PASSES):
@@ -116,20 +102,22 @@ def tile_picked_zlateq_gelu_p_kernel(tc, x_words, x_scales, w1, v_words, v_scale
             w_codes.append(codes)
             w_scales.append(scales)
             if o == 0:
-                warm_up(codes[:, :P], scales[:, :P])
-                pick_words(0)
+                pick_words(0, (0, 2 * P, S))
 
         vw_tab = keep.tile([P, G], I32, name="vw_tab", tag="w_raw0", align_bytes=64)
         load_words(vw_tab, v_words[0])
         for r in range(ROWS):
             nc.sync.dma_start(out=vs[V_PLANE + r : P : QUAD, :].bitcast(I32), in_=vs_spread[FIRST + SPREAD * r : FIRST + 15 * SPREAD + 1 : ROWS * SPREAD, :].bitcast(I32))
 
-        pick_words(1)
+        pick_words(1, (0, P, 2 * P, S))
 
         h_bf = keep.tile([P, S * PACK], BF16, name="h_bf", align_bytes=64)
         h_scales = keep.tile([P, S], U8, name="h_scales", align_bytes=64)
         h_codes = keep.tile([P, S], U32, name="h_codes", align_bytes=64)
-        accs = [psum.tile([P, BANK], F32, name="acc") for b in range(S // P)]
+        accs = []
+
+        def bank(n):
+            return psum.tile([P, BANK], F32, name="bank%d" % n, tag="bank%d" % n)
 
         def project(o, b):
             for t in range(PACK):
@@ -144,25 +132,26 @@ def tile_picked_zlateq_gelu_p_kernel(tc, x_words, x_scales, w1, v_words, v_scale
                     stop=(o == PASSES - 1 and t == PACK - 1),
                 )
 
-        for b in range(S // P):
+        for b in range(BLOCKS - 1):
+            accs.append(bank(b))
             project(0, b)
-        for b in range(S // P):
+        for b in range(BLOCKS):
             tok = slice(b * P, (b + 1) * P)
-            acc = accs[b]
+            if b == BLOCKS - 1:
+                accs.append(bank(0))
+                project(0, b)
             project(1, b)
             block = h_bf[:, b * K_PASS : (b + 1) * K_PASS]
             nc.scalar.activation(
-                block.rearrange("p (n t) -> p n t", t=PACK), acc[:].rearrange("p (t n) -> p n t", t=PACK), GELU
+                block.rearrange("p (n t) -> p n t", t=PACK), accs[b][:].rearrange("p (t n) -> p n t", t=PACK), GELU
             )
             nc.vector.quantize_mx(out=h_codes[:, tok].bitcast(FP8X4), scales=h_scales[:, tok], in_=block)
-            if b == 2:
-                warm_up(h_codes[:, tok], h_scales[:, tok])
 
-        vw = [keep.tile([P, BANK], U32, name="vw%d" % g, align_bytes=64) for g in range(V // BANK)]
-        for g in range(V // BANK):
-            nc.vector.tensor_copy(
-                vw[g][:], vw_tab[:].bitcast(U32).indirect(doc_t[:, g * BANK // LIST : (g + 1) * BANK // LIST])
-            )
+        pieces = [(0, BANK // 2), (BANK // 2, BANK), (BANK, V)]
+        vw = []
+        for n, (lo, hi) in enumerate(pieces):
+            vw.append(keep.tile([P, hi - lo], U32, name="vw%d" % n, align_bytes=64))
+            pick(vw[n][:], vw_tab, doc_t, lo, hi)
 
         docs = BANK // D
         blocks = S // P
@@ -171,18 +160,29 @@ def tile_picked_zlateq_gelu_p_kernel(tc, x_words, x_scales, w1, v_words, v_scale
         pairs = [keep.tile([P, len(part), R, 2], F32, name="pairs%d" % n, tag="pairs%d" % n, align_bytes=64) for n, part in enumerate(parts)]
         best = [keep.tile([P, len(part), R], F32, name="best%d" % n, align_bytes=64) for n, part in enumerate(parts)]
 
-        def score(g, b):
-            acc = psum.tile([P, BANK], F32, name="acc")
+        banks = {}
+
+        def score_pass(n, b):
+            lo, hi = pieces[n]
+            g, at = divmod(lo, BANK)
+            if (g, b) not in banks:
+                banks[(g, b)] = bank(4 * (1 - g) + b)
             nc.tensor.matmul_mx(
-                out=acc[:],
+                out=banks[(g, b)][:, at : at + hi - lo],
                 lhsT=h_codes[:, b * P : (b + 1) * P].bitcast(FP8X4),
                 lhsT_scale=h_scales[:, b * P : (b + 1) * P],
-                rhs=vw[g][:].bitcast(FP8X4),
-                rhs_scale=vs[V_PLANE:P, g * BANK : (g + 1) * BANK],
+                rhs=vw[n][:].bitcast(FP8X4),
+                rhs_scale=vs[V_PLANE:P, lo:hi],
                 start=True,
                 stop=True,
             )
-            return acc[:].rearrange("p (v d) -> p v d", d=D)
+
+        for b in range(blocks):
+            score_pass(0, b)
+
+        def score(g, b):
+            score_pass(g + 1, b)
+            return banks[(g, b)][:].rearrange("p (v d) -> p v d", d=D)
 
         def reduce_whole(g, b, tag):
             whole = keep.tile([P, docs], F32, name="whole%d" % g, tag=tag, align_bytes=64)

@@ -78,7 +78,7 @@ def tile_picked_zlateq_gelu_p_kernel(tc, x_words, x_scales, w1, v_words, v_scale
             nc.sync.dma_start(out=xs[r:P:QUAD, :].bitcast(I32), in_=xs_spread[FIRST + SPREAD * r : FIRST + 15 * SPREAD + 1 : ROWS * SPREAD, :].bitcast(I32))
         xw_tab.append(keep.tile([P, T], I32, name="xw_tab1", tag="xs_tab", align_bytes=64))
         load_words(xw_tab[1], x_words[1])
-        vs_spread = keep.tile([P, V], U8, name="vs_spread", align_bytes=64)
+        vs_spread = keep.tile([P, V], U8, name="vs_spread", tag="vs_spread", align_bytes=64)
         nc.vector.tensor_copy(vs_spread[:], vs_tab[:].indirect(doc_t[:]))
 
         xw = [keep.tile([P, S], U32, name="xw%d" % o, align_bytes=64) for o in range(PASSES)]
@@ -112,8 +112,7 @@ def tile_picked_zlateq_gelu_p_kernel(tc, x_words, x_scales, w1, v_words, v_scale
         pick_words(1, (0, P, 2 * P, S))
 
         h_bf = keep.tile([P, S * PACK], BF16, name="h_bf", align_bytes=64)
-        h_scales = keep.tile([P, S], U8, name="h_scales", align_bytes=64)
-        h_codes = keep.tile([P, S], U32, name="h_codes", align_bytes=64)
+        h_codes, h_scales = [], []
         accs = []
 
         def bank(n):
@@ -136,16 +135,18 @@ def tile_picked_zlateq_gelu_p_kernel(tc, x_words, x_scales, w1, v_words, v_scale
             accs.append(bank(b))
             project(0, b)
         for b in range(BLOCKS):
-            tok = slice(b * P, (b + 1) * P)
             if b == BLOCKS - 1:
-                accs.append(bank(0))
+                accs.append(bank(b - 1))
                 project(0, b)
             project(1, b)
             block = h_bf[:, b * K_PASS : (b + 1) * K_PASS]
             nc.scalar.activation(
                 block.rearrange("p (n t) -> p n t", t=PACK), accs[b][:].rearrange("p (t n) -> p n t", t=PACK), GELU
             )
-            nc.vector.quantize_mx(out=h_codes[:, tok].bitcast(FP8X4), scales=h_scales[:, tok], in_=block)
+            h_codes.append(keep.tile([P, P], U32, name="h_codes%d" % b, align_bytes=64))
+            tag = "vs_spread" if b == BLOCKS - 1 else "h_scales%d" % b
+            h_scales.append(keep.tile([P, P], U8, name="h_scales%d" % b, tag=tag, align_bytes=64))
+            nc.vector.quantize_mx(out=h_codes[b][:].bitcast(FP8X4), scales=h_scales[b][:], in_=block)
 
         pieces = [(0, BANK // 2), (BANK // 2, BANK), (BANK, V)]
         vw = []
@@ -169,18 +170,20 @@ def tile_picked_zlateq_gelu_p_kernel(tc, x_words, x_scales, w1, v_words, v_scale
                 banks[(g, b)] = bank(4 * (1 - g) + b)
             nc.tensor.matmul_mx(
                 out=banks[(g, b)][:, at : at + hi - lo],
-                lhsT=h_codes[:, b * P : (b + 1) * P].bitcast(FP8X4),
-                lhsT_scale=h_scales[:, b * P : (b + 1) * P],
+                lhsT=h_codes[b][:].bitcast(FP8X4),
+                lhsT_scale=h_scales[b][:],
                 rhs=vw[n][:].bitcast(FP8X4),
                 rhs_scale=vs[V_PLANE:P, lo:hi],
                 start=True,
                 stop=True,
             )
 
-        for b in range(blocks):
+        for b in range(blocks - 1):
             score_pass(0, b)
 
         def score(g, b):
+            if (g, b) == (0, blocks - 1):
+                score_pass(0, b)
             score_pass(g + 1, b)
             return banks[(g, b)][:].rearrange("p (v d) -> p v d", d=D)
 
@@ -201,10 +204,14 @@ def tile_picked_zlateq_gelu_p_kernel(tc, x_words, x_scales, w1, v_words, v_scale
             mine = quads[:, parts[n].start - 1 : parts[n].stop - 1, cols, :]
             nc.vector.tensor_tensor(pairs[n][:, :, cols, :], mine[:, :, :, :2], mine[:, :, :, 2:], MAX)
 
-        for g in range(V // BANK):
-            for b in range(1, blocks):
-                reduce_half(g, b)
-            halve(0, slice(g * docs, (g + 1) * docs))
+        reduce_half(0, 1)
+        reduce_half(0, 2)
+        reduce_half(1, 1)
+        halve(0, slice(0, docs))
+        reduce_half(1, 2)
+        reduce_half(0, 3)
+        reduce_half(1, 3)
+        halve(0, slice(docs, R))
         halve(1, slice(0, R))
         for n, part in enumerate(parts):
             nc.vector.tensor_tensor(best[n][:], pairs[n][:, :, :, 0], pairs[n][:, :, :, 1], MAX)

@@ -17,15 +17,16 @@ MAX = mybir.AluOpType.max
 AXIS_X = mybir.AxisListType.X
 
 P = 128
+HALF = P // 2
 PACK = 4
 K_PASS = P * PACK
 PASSES = K // K_PASS
-QUADS = 4
 QUAD = 32
 ROWS = 4
-SPREAD = 7
-FIRST = 17
-TABLE_ROWS = slice(FIRST, FIRST + 15 * SPREAD + 1, SPREAD)
+X_STEP = 4
+V_STEP = 7
+V_FIRST = 17
+V_ROWS = slice(V_FIRST, V_FIRST + 15 * V_STEP + 1, V_STEP)
 V_PLANE = 8
 BANK = 512
 LIST = 16
@@ -36,11 +37,12 @@ def tile_picked_zlateq_gelu_p_kernel(tc, x_words, x_scales, w1, v_words, v_scale
     nc = tc.nc
     with ExitStack() as ctx:
         keep = ctx.enter_context(tc.tile_pool(name="keep", bufs=1))
+        placed = ctx.enter_context(tc.tile_pool(name="placed", bufs=1))
         psum = ctx.enter_context(tc.psum_pool(name="psum", bufs=1))
 
         offs_t = keep.tile([P, S // LIST], U16, name="offs_t")
         doc_t = keep.tile([P, V // LIST], U16, name="doc_t")
-        xs_tab = keep.tile([P, PASSES * T], U8, name="xs_tab", tag="xs_tab", align_bytes=64)
+        xs_tab = keep.tile([P, T], U8, name="xs_tab", tag="xs_tab", align_bytes=64)
         vs_tab = keep.tile([P, G], U8, name="vs_tab", tag="vs_tab", align_bytes=64)
         vs = keep.tile([P, V], U8, name="vs", align_bytes=64)
         xs = keep.tile([P, PASSES * S], U8, name="xs", align_bytes=64)
@@ -51,9 +53,7 @@ def tile_picked_zlateq_gelu_p_kernel(tc, x_words, x_scales, w1, v_words, v_scale
         def load_words(tab, words):
             nc.sync.dma_start(out=tab[:], in_=words.rearrange("p n t -> p (n t)").bitcast(I32))
 
-        nc.vector.memset(xs_tab[:, :T].bitcast(I32), 0)
-        nc.gpsimd.memset(xs_tab[:, T:].bitcast(I32), 0)
-        for tile in (vs_tab, xs, vs):
+        for tile in (xs_tab, vs_tab, xs, vs):
             nc.vector.memset(tile[:].bitcast(I32), 0)
         warm_in = keep.tile([P, 1], F32, name="warm_in")
         warm_out = keep.tile([P, 1], F32, name="warm_out")
@@ -61,25 +61,28 @@ def tile_picked_zlateq_gelu_p_kernel(tc, x_words, x_scales, w1, v_words, v_scale
         nc.scalar.activation(warm_out[:], warm_in[:], GELU)
         nc.sync.dma_start(out=w_raw[0][:, :2, :], in_=w_rows[0][:, :2, :])
         nc.sync.dma_start(offs_t[:], offs)
-        nc.sync.dma_start(doc_t[:], doc)
-        nc.sync.dma_start(
-            out=xs_tab[TABLE_ROWS, :].bitcast(I32).rearrange("r (o c) -> r o c", o=PASSES),
-            in_=x_scales.bitcast(I32).rearrange("o r c -> r o c"),
-        )
+        nc.sync.dma_start(out=xs_tab[0:P:X_STEP, :].bitcast(I32), in_=x_scales.bitcast(I32).rearrange("o r c -> (o r) c"))
         nc.sync.dma_start(out=w_raw[0][:, 2:, :], in_=w_rows[0][:, 2:, :])
-        nc.sync.dma_start(out=vs_tab[TABLE_ROWS, :].bitcast(I32), in_=v_scales[0].bitcast(I32))
+        nc.sync.dma_start(doc_t[:], doc)
+        nc.sync.dma_start(out=vs_tab[V_ROWS, :].bitcast(I32), in_=v_scales[0].bitcast(I32))
         nc.sync.dma_start(out=w_raw[1][:], in_=w_rows[1])
         load_words(xw_tab[0], x_words[0])
 
-        xs_spread = keep.tile([P, PASSES * S], U8, name="xs_spread", align_bytes=64)
-        for o in range(PASSES):
-            nc.vector.tensor_copy(xs_spread[:, o * S : (o + 1) * S], xs_tab[:, o * T : (o + 1) * T].indirect(offs_t[:]))
+        xs_picked = placed.tile([P, S], U8, name="xs_picked", offset=4 * T - 64, align_bytes=64)
+        nc.vector.tensor_copy(xs_picked[:], xs_tab[:].indirect(offs_t[:]))
+        xs_folded = keep.tile([HALF, PASSES * S], U8, name="xs_folded", align_bytes=64)
+        for o in reversed(range(PASSES)):
+            nc.vector.tensor_copy(xs_folded[:, o * S : (o + 1) * S].bitcast(I32), xs_picked[o * HALF : (o + 1) * HALF, :].bitcast(I32))
         for r in range(ROWS):
-            nc.sync.dma_start(out=xs[r:P:QUAD, :].bitcast(I32), in_=xs_spread[FIRST + SPREAD * r : FIRST + 15 * SPREAD + 1 : ROWS * SPREAD, :].bitcast(I32))
-        xw_tab.append(keep.tile([P, T], I32, name="xw_tab1", tag="xs_tab", align_bytes=64))
+            nc.sync.dma_start(out=xs[r:P:QUAD, :].bitcast(I32), in_=xs_folded[X_STEP * r : HALF : ROWS * X_STEP, :].bitcast(I32))
+        xw_tab.append(placed.tile([P, T], I32, name="xw_tab1", offset=0, align_bytes=64))
         load_words(xw_tab[1], x_words[1])
-        vs_spread = keep.tile([P, V], U8, name="vs_spread", tag="vs_spread", align_bytes=64)
-        nc.vector.tensor_copy(vs_spread[:], vs_tab[:].indirect(doc_t[:]))
+        vw_tab = placed.tile([P, G], I32, name="vw_tab", offset=4 * T + S - 128, align_bytes=64)
+        load_words(vw_tab, v_words[0])
+        vs_picked = keep.tile([P, V], U8, name="vs_picked", tag="xs_tab", align_bytes=64)
+        nc.vector.tensor_copy(vs_picked[:], vs_tab[:].indirect(doc_t[:]))
+        for r in range(ROWS):
+            nc.sync.dma_start(out=vs[V_PLANE + r : P : QUAD, :].bitcast(I32), in_=vs_picked[V_FIRST + V_STEP * r : V_ROWS.stop : ROWS * V_STEP, :].bitcast(I32))
 
         xw = [keep.tile([P, S], U32, name="xw%d" % o, align_bytes=64) for o in range(PASSES)]
 
@@ -97,26 +100,21 @@ def tile_picked_zlateq_gelu_p_kernel(tc, x_words, x_scales, w1, v_words, v_scale
             src = w_raw[o][:].rearrange("p j (m t) -> p m j t", t=PACK)
             nc.scalar.copy(dst, src)
             codes = keep.tile([P, H], U32, name="w_codes%d" % o, align_bytes=64)
-            scales = keep.tile([P, H], U8, name="w_scales%d" % o, tag="w_scales0" if o == 0 else "xw_tab0", align_bytes=64)
+            scales = keep.tile([P, H], U8, name="w_scales%d" % o, tag="vs_tab" if o == 0 else "xw_tab0", align_bytes=64)
             nc.vector.quantize_mx(out=codes[:].bitcast(FP8X4), scales=scales[:], in_=grouped[:])
             w_codes.append(codes)
             w_scales.append(scales)
             if o == 0:
-                pick_words(0, (0, 2 * P, S))
-
-        vw_tab = keep.tile([P, G], I32, name="vw_tab", tag="w_raw0", align_bytes=64)
-        load_words(vw_tab, v_words[0])
-        for r in range(ROWS):
-            nc.sync.dma_start(out=vs[V_PLANE + r : P : QUAD, :].bitcast(I32), in_=vs_spread[FIRST + SPREAD * r : FIRST + 15 * SPREAD + 1 : ROWS * SPREAD, :].bitcast(I32))
-
+                pick_words(0, (0, P, 2 * P, S))
         pick_words(1, (0, P, 2 * P, S))
 
         h_bf = keep.tile([P, S * PACK], BF16, name="h_bf", align_bytes=64)
         h_codes, h_scales = [], []
-        accs = []
 
         def bank(n):
             return psum.tile([P, BANK], F32, name="bank%d" % n, tag="bank%d" % n)
+
+        accs = [bank(b) for b in range(BLOCKS - 1)]
 
         def project(o, b):
             for t in range(PACK):
@@ -132,11 +130,10 @@ def tile_picked_zlateq_gelu_p_kernel(tc, x_words, x_scales, w1, v_words, v_scale
                 )
 
         for b in range(BLOCKS - 1):
-            accs.append(bank(b))
             project(0, b)
         for b in range(BLOCKS):
             if b == BLOCKS - 1:
-                accs.append(bank(b - 1))
+                accs.append(bank(0))
                 project(0, b)
             project(1, b)
             block = h_bf[:, b * K_PASS : (b + 1) * K_PASS]
@@ -144,73 +141,66 @@ def tile_picked_zlateq_gelu_p_kernel(tc, x_words, x_scales, w1, v_words, v_scale
                 block.rearrange("p (n t) -> p n t", t=PACK), accs[b][:].rearrange("p (t n) -> p n t", t=PACK), GELU
             )
             h_codes.append(keep.tile([P, P], U32, name="h_codes%d" % b, align_bytes=64))
-            tag = "vs_spread" if b == BLOCKS - 1 else "h_scales%d" % b
-            h_scales.append(keep.tile([P, P], U8, name="h_scales%d" % b, tag=tag, align_bytes=64))
+            h_scales.append(keep.tile([P, P], U8, name="h_scales%d" % b, align_bytes=64))
             nc.vector.quantize_mx(out=h_codes[b][:].bitcast(FP8X4), scales=h_scales[b][:], in_=block)
 
-        pieces = [(0, BANK // 2), (BANK // 2, BANK), (BANK, V)]
-        vw = []
-        for n, (lo, hi) in enumerate(pieces):
-            vw.append(keep.tile([P, hi - lo], U32, name="vw%d" % n, align_bytes=64))
-            pick(vw[n][:], vw_tab, doc_t, lo, hi)
+        vw = [keep.tile([P, BANK], U32, name="vw%d" % g, tag="vw%d" % g, align_bytes=64) for g in range(V // BANK)]
+        for lo, hi in ((0, BANK // 2), (BANK // 2, BANK), (BANK, V)):
+            pick(vw[lo // BANK][:, lo % BANK : lo % BANK + hi - lo], vw_tab, doc_t, lo, hi)
 
         docs = BANK // D
-        blocks = S // P
         parts = [range(1, 3), range(3, 4)]
-        quads = keep.tile([P, blocks - 1, R, 4], F32, name="quads", tag="quads", align_bytes=64)
-        pairs = [keep.tile([P, len(part), R, 2], F32, name="pairs%d" % n, tag="pairs%d" % n, align_bytes=64) for n, part in enumerate(parts)]
+        quads = keep.tile([P, BLOCKS - 1, R, 4], F32, name="quads", tag="quads", align_bytes=64)
+        pairs = [keep.tile([P, len(part), R, 2], F32, name="pairs%d" % n, tag="vw0" if n == 0 else "pairs1", align_bytes=64) for n, part in enumerate(parts)]
         best = [keep.tile([P, len(part), R], F32, name="best%d" % n, align_bytes=64) for n, part in enumerate(parts)]
 
         banks = {}
 
-        def score_pass(n, b):
-            lo, hi = pieces[n]
-            g, at = divmod(lo, BANK)
+        def score_pass(g, b, lo=0, hi=BANK):
             if (g, b) not in banks:
-                banks[(g, b)] = bank(4 * (1 - g) + b)
+                banks[(g, b)] = bank(BLOCKS * (1 - g) + b)
             nc.tensor.matmul_mx(
-                out=banks[(g, b)][:, at : at + hi - lo],
+                out=banks[(g, b)][:, lo:hi],
                 lhsT=h_codes[b][:].bitcast(FP8X4),
                 lhsT_scale=h_scales[b][:],
-                rhs=vw[n][:].bitcast(FP8X4),
-                rhs_scale=vs[V_PLANE:P, lo:hi],
+                rhs=vw[g][:, lo:hi].bitcast(FP8X4),
+                rhs_scale=vs[V_PLANE:P, g * BANK + lo : g * BANK + hi],
                 start=True,
                 stop=True,
             )
 
-        for b in range(blocks - 1):
-            score_pass(0, b)
-
-        def score(g, b):
-            if (g, b) == (0, blocks - 1):
-                score_pass(0, b)
-            score_pass(g + 1, b)
+        def scores_of(g, b):
             return banks[(g, b)][:].rearrange("p (v d) -> p v d", d=D)
 
         def reduce_whole(g, b, tag):
             whole = keep.tile([P, docs], F32, name="whole%d" % g, tag=tag, align_bytes=64)
-            nc.vector.tensor_reduce(whole[:], score(g, b), AXIS_X, MAX)
+            nc.vector.tensor_reduce(whole[:], scores_of(g, b), AXIS_X, MAX)
             nc.sync.dma_start(out=out[b * P : (b + 1) * P, g * docs : (g + 1) * docs], in_=whole[:])
 
         def reduce_half(g, b):
-            scores = score(g, b)
+            scores = scores_of(g, b)
             upper = keep.tile([P, docs, 4], F32, name="upper%d_%d" % (g, b), align_bytes=64)
             nc.scalar.copy(upper[:], scores[:, :, 4:])
             nc.vector.tensor_tensor(quads[:, b - 1, g * docs : (g + 1) * docs, :], scores[:, :, :4], upper[:], MAX)
-
-        reduce_whole(0, 0, "whole0")
 
         def halve(n, cols):
             mine = quads[:, parts[n].start - 1 : parts[n].stop - 1, cols, :]
             nc.vector.tensor_tensor(pairs[n][:, :, cols, :], mine[:, :, :, :2], mine[:, :, :, 2:], MAX)
 
-        reduce_half(0, 1)
-        reduce_half(0, 2)
-        reduce_half(1, 1)
+        for lo in (0, BANK // 2):
+            for b in parts[0]:
+                score_pass(0, b, lo, lo + BANK // 2)
+        score_pass(0, 0)
+        score_pass(0, BLOCKS - 1)
+        for b in parts[0]:
+            reduce_half(0, b)
+        reduce_whole(0, 0, "whole0")
         halve(0, slice(0, docs))
-        reduce_half(1, 2)
-        reduce_half(0, 3)
-        reduce_half(1, 3)
+        reduce_half(0, BLOCKS - 1)
+        for b in range(1, BLOCKS):
+            score_pass(1, b)
+            reduce_half(1, b)
+        score_pass(1, 0)
         halve(0, slice(docs, R))
         halve(1, slice(0, R))
         for n, part in enumerate(parts):

@@ -31,6 +31,7 @@ V_PLANE = 8
 BANK = 512
 LIST = 16
 BLOCKS = S // P
+WARM_M = 32
 
 
 def tile_picked_zlateq_gelu_p_kernel(tc, x_words, x_scales, w1, v_words, v_scales, offs, doc, out):
@@ -108,6 +109,22 @@ def tile_picked_zlateq_gelu_p_kernel(tc, x_words, x_scales, w1, v_words, v_scale
                 pick_words(0, (0, P, 2 * P, S))
         pick_words(1, (0, P, 2 * P, S))
 
+        warm_bank = psum.tile([P, BANK], F32, name="bank3", tag="bank3")
+
+        def warm_up(codes, scales):
+            nc.tensor.matmul_mx(
+                out=warm_bank[:WARM_M, :],
+                lhsT=codes[:, :WARM_M].bitcast(FP8X4),
+                lhsT_scale=scales[:, :WARM_M],
+                rhs=w_codes[0][:].bitcast(FP8X4),
+                rhs_scale=w_scales[0][:],
+                start=True,
+                stop=True,
+            )
+
+        for n in range(2):
+            warm_up(w_codes[0], w_scales[0])
+
         h_bf = keep.tile([P, S * PACK], BF16, name="h_bf", align_bytes=64)
         h_codes, h_scales = [], []
 
@@ -143,6 +160,8 @@ def tile_picked_zlateq_gelu_p_kernel(tc, x_words, x_scales, w1, v_words, v_scale
             h_codes.append(keep.tile([P, P], U32, name="h_codes%d" % b, align_bytes=64))
             h_scales.append(keep.tile([P, P], U8, name="h_scales%d" % b, align_bytes=64))
             nc.vector.quantize_mx(out=h_codes[b][:].bitcast(FP8X4), scales=h_scales[b][:], in_=block)
+        for b in (BLOCKS - 2, BLOCKS - 1, BLOCKS - 1):
+            warm_up(h_codes[b], h_scales[b])
 
         vw = [keep.tile([P, BANK], U32, name="vw%d" % g, tag="vw%d" % g, align_bytes=64) for g in range(V // BANK)]
         for lo, hi in ((0, BANK // 2), (BANK // 2, BANK), (BANK, V)):

@@ -160,12 +160,12 @@ def tile_picked_zlateq_gelu_p_kernel(tc, x_words, x_scales, w1, v_words, v_scale
             h_codes.append(keep.tile([P, P], U32, name="h_codes%d" % b, align_bytes=64))
             h_scales.append(keep.tile([P, P], U8, name="h_scales%d" % b, align_bytes=64))
             nc.vector.quantize_mx(out=h_codes[b][:].bitcast(FP8X4), scales=h_scales[b][:], in_=block)
-        for b in (BLOCKS - 2, BLOCKS - 1, BLOCKS - 1):
+        for b in (BLOCKS - 2, BLOCKS - 2, BLOCKS - 1, BLOCKS - 1):
             warm_up(h_codes[b], h_scales[b])
 
         vw = [keep.tile([P, BANK], U32, name="vw%d" % g, tag="vw%d" % g, align_bytes=64) for g in range(V // BANK)]
-        for lo, hi in ((0, BANK // 2), (BANK // 2, BANK), (BANK, V)):
-            pick(vw[lo // BANK][:, lo % BANK : lo % BANK + hi - lo], vw_tab, doc_t, lo, hi)
+        for g in range(V // BANK):
+            pick(vw[g][:], vw_tab, doc_t, g * BANK, (g + 1) * BANK)
 
         docs = BANK // D
         parts = [range(1, 3), range(3, 4)]
@@ -175,15 +175,14 @@ def tile_picked_zlateq_gelu_p_kernel(tc, x_words, x_scales, w1, v_words, v_scale
 
         banks = {}
 
-        def score_pass(g, b, lo=0, hi=BANK):
-            if (g, b) not in banks:
-                banks[(g, b)] = bank(BLOCKS * (1 - g) + b)
+        def score_pass(g, b):
+            banks[(g, b)] = bank(BLOCKS * (1 - g) + b)
             nc.tensor.matmul_mx(
-                out=banks[(g, b)][:, lo:hi],
+                out=banks[(g, b)][:],
                 lhsT=h_codes[b][:].bitcast(FP8X4),
                 lhsT_scale=h_scales[b][:],
-                rhs=vw[g][:, lo:hi].bitcast(FP8X4),
-                rhs_scale=vs[V_PLANE:P, g * BANK + lo : g * BANK + hi],
+                rhs=vw[g][:].bitcast(FP8X4),
+                rhs_scale=vs[V_PLANE:P, g * BANK : (g + 1) * BANK],
                 start=True,
                 stop=True,
             )
@@ -206,16 +205,12 @@ def tile_picked_zlateq_gelu_p_kernel(tc, x_words, x_scales, w1, v_words, v_scale
             mine = quads[:, parts[n].start - 1 : parts[n].stop - 1, cols, :]
             nc.vector.tensor_tensor(pairs[n][:, :, cols, :], mine[:, :, :, :2], mine[:, :, :, 2:], MAX)
 
-        for lo in (0, BANK // 2):
-            for b in parts[0]:
-                score_pass(0, b, lo, lo + BANK // 2)
-        score_pass(0, 0)
-        score_pass(0, BLOCKS - 1)
-        for b in parts[0]:
-            reduce_half(0, b)
+        for b in range(BLOCKS):
+            score_pass(0, b)
         reduce_whole(0, 0, "whole0")
+        for b in range(1, BLOCKS):
+            reduce_half(0, b)
         halve(0, slice(0, docs))
-        reduce_half(0, BLOCKS - 1)
         for b in range(1, BLOCKS):
             score_pass(1, b)
             reduce_half(1, b)

@@ -24,8 +24,8 @@ PASSES = K // K_PASS
 QUAD = 32
 ROWS = 4
 X_STEP = 4
-V_STEP = 7
-V_FIRST = 17
+V_STEP = 4
+V_FIRST = 32
 V_ROWS = slice(V_FIRST, V_FIRST + 15 * V_STEP + 1, V_STEP)
 V_PLANE = 8
 BANK = 512

@@ -169,8 +169,8 @@ def tile_picked_zlateq_gelu_p_kernel(tc, x_words, x_scales, w1, v_words, v_scale
 
         docs = BANK // D
         parts = [range(1, 3), range(3, 4)]
-        quads = keep.tile([P, BLOCKS - 1, R, 4], F32, name="quads", tag="quads", align_bytes=64)
-        pairs = [keep.tile([P, len(part), R, 2], F32, name="pairs%d" % n, tag="vw0" if n == 0 else "pairs1", align_bytes=64) for n, part in enumerate(parts)]
+        quads = keep.tile([P, BLOCKS - 1, 4, R], F32, name="quads", tag="quads", align_bytes=64)
+        pairs = [keep.tile([P, len(part), 2, R], F32, name="pairs%d" % n, tag="vw0" if n == 0 else "pairs1", align_bytes=64) for n, part in enumerate(parts)]
         best = [keep.tile([P, len(part), R], F32, name="best%d" % n, align_bytes=64) for n, part in enumerate(parts)]
 
         banks = {}
@@ -196,14 +196,14 @@ def tile_picked_zlateq_gelu_p_kernel(tc, x_words, x_scales, w1, v_words, v_scale
             nc.sync.dma_start(out=out[b * P : (b + 1) * P, g * docs : (g + 1) * docs], in_=whole[:])
 
         def reduce_half(g, b):
-            scores = scores_of(g, b)
-            upper = keep.tile([P, docs, 4], F32, name="upper%d_%d" % (g, b), align_bytes=64)
-            nc.scalar.copy(upper[:], scores[:, :, 4:])
-            nc.vector.tensor_tensor(quads[:, b - 1, g * docs : (g + 1) * docs, :], scores[:, :, :4], upper[:], MAX)
+            scores = banks[(g, b)][:].rearrange("p (v d) -> p d v", d=D)
+            upper = keep.tile([P, 4, docs], F32, name="upper%d_%d" % (g, b), align_bytes=64)
+            nc.scalar.copy(upper[:], scores[:, 4:, :])
+            nc.vector.tensor_tensor(quads[:, b - 1, :, g * docs : (g + 1) * docs], scores[:, :4, :], upper[:], MAX)
 
         def halve(n, cols):
-            mine = quads[:, parts[n].start - 1 : parts[n].stop - 1, cols, :]
-            nc.vector.tensor_tensor(pairs[n][:, :, cols, :], mine[:, :, :, :2], mine[:, :, :, 2:], MAX)
+            mine = quads[:, parts[n].start - 1 : parts[n].stop - 1, :, cols]
+            nc.vector.tensor_tensor(pairs[n][:, :, :, cols], mine[:, :, :2, :], mine[:, :, 2:, :], MAX)
 
         for b in range(BLOCKS):
             score_pass(0, b)
@@ -218,7 +218,7 @@ def tile_picked_zlateq_gelu_p_kernel(tc, x_words, x_scales, w1, v_words, v_scale
         halve(0, slice(docs, R))
         halve(1, slice(0, R))
         for n, part in enumerate(parts):
-            nc.vector.tensor_tensor(best[n][:], pairs[n][:, :, :, 0], pairs[n][:, :, :, 1], MAX)
+            nc.vector.tensor_tensor(best[n][:], pairs[n][:, :, 0, :], pairs[n][:, :, 1, :], MAX)
             for b in part:
                 nc.sync.dma_start(out=out[b * P : (b + 1) * P, :], in_=best[n][:, b - part.start, :])
         reduce_whole(1, 0, "quads")

from contextlib import ExitStack

import concourse.mybir as mybir

K, T, S, D, H, V, G, R = 1024, 2048, 512, 8, 512, 1024, 4096, 128
FLOPS = 2 * K * H * S + 2 * H * S * V

F32 = mybir.dt.float32
BF16 = mybir.dt.bfloat16
I32 = mybir.dt.int32
U32 = mybir.dt.uint32
U16 = mybir.dt.uint16
U8 = mybir.dt.uint8
FP8X4 = mybir.dt.float8_e4m3fn_x4
GELU = mybir.ActivationFunctionType.Gelu_apprx_tanh
MAX = mybir.AluOpType.max
AXIS_X = mybir.AxisListType.X

P = 128
HALF = P // 2
PACK = 4
K_PASS = P * PACK
PASSES = K // K_PASS
QUAD = 32
ROWS = 4
X_STEP = 4
V_STEP = 4
V_FIRST = 32
V_ROWS = slice(V_FIRST, V_FIRST + 15 * V_STEP + 1, V_STEP)
V_PLANE = 8
BANK = 512
LIST = 16
BLOCKS = S // P
WARM_M = 32


def tile_picked_zlateq_gelu_p_kernel(tc, x_words, x_scales, w1, v_words, v_scales, offs, doc, out):
    nc = tc.nc
    with ExitStack() as ctx:
        keep = ctx.enter_context(tc.tile_pool(name="keep", bufs=1))
        placed = ctx.enter_context(tc.tile_pool(name="placed", bufs=1))
        psum = ctx.enter_context(tc.psum_pool(name="psum", bufs=1))

        offs_t = keep.tile([P, S // LIST], U16, name="offs_t")
        doc_t = keep.tile([P, V // LIST], U16, name="doc_t")
        xs_tab = keep.tile([P, T], U8, name="xs_tab", tag="xs_tab", align_bytes=64)
        vs_tab = keep.tile([P, G], U8, name="vs_tab", tag="vs_tab", align_bytes=64)
        vs = keep.tile([P, V], U8, name="vs", align_bytes=64)
        xs = keep.tile([P, PASSES * S], U8, name="xs", align_bytes=64)
        xw_tab = [keep.tile([P, T], I32, name="xw_tab0", tag="xw_tab0", align_bytes=64)]
        w_raw = [keep.tile([P, PACK, H], F32, name="w_raw%d" % o, tag="w_raw%d" % o, align_bytes=64) for o in range(PASSES)]
        w_rows = [w1[o * K_PASS : (o + 1) * K_PASS, :].rearrange("(p j) c -> p j c", j=PACK) for o in range(PASSES)]

        def load_words(tab, words):
            nc.sync.dma_start(out=tab[:], in_=words.rearrange("p n t -> p (n t)").bitcast(I32))

        for tile in (xs_tab, vs_tab, xs, vs):
            nc.vector.memset(tile[:].bitcast(I32), 0)
        warm_in = keep.tile([P, 1], F32, name="warm_in")
        warm_out = keep.tile([P, 1], F32, name="warm_out")
        nc.vector.memset(warm_in[:], 0.0)
        nc.scalar.activation(warm_out[:], warm_in[:], GELU)
        nc.sync.dma_start(out=w_raw[0][:, :2, :], in_=w_rows[0][:, :2, :])
        nc.sync.dma_start(offs_t[:], offs)
        nc.sync.dma_start(out=xs_tab[0:P:X_STEP, :].bitcast(I32), in_=x_scales.bitcast(I32).rearrange("o r c -> (o r) c"))
        nc.sync.dma_start(out=w_raw[0][:, 2:, :], in_=w_rows[0][:, 2:, :])
        nc.sync.dma_start(doc_t[:], doc)
        nc.sync.dma_start(out=vs_tab[V_ROWS, :].bitcast(I32), in_=v_scales[0].bitcast(I32))
        nc.sync.dma_start(out=w_raw[1][:], in_=w_rows[1])
        load_words(xw_tab[0], x_words[0])

        xs_picked = placed.tile([P, S], U8, name="xs_picked", offset=4 * T - 64, align_bytes=64)
        nc.vector.tensor_copy(xs_picked[:], xs_tab[:].indirect(offs_t[:]))
        xs_folded = keep.tile([HALF, PASSES * S], U8, name="xs_folded", align_bytes=64)
        for o in reversed(range(PASSES)):
            nc.vector.tensor_copy(xs_folded[:, o * S : (o + 1) * S].bitcast(I32), xs_picked[o * HALF : (o + 1) * HALF, :].bitcast(I32))
        for r in range(ROWS):
            nc.sync.dma_start(out=xs[r:P:QUAD, :].bitcast(I32), in_=xs_folded[X_STEP * r : HALF : ROWS * X_STEP, :].bitcast(I32))
        xw_tab.append(placed.tile([P, T], I32, name="xw_tab1", offset=0, align_bytes=64))
        load_words(xw_tab[1], x_words[1])
        vw_tab = placed.tile([P, G], I32, name="vw_tab", offset=4 * T + S - 128, align_bytes=64)
        load_words(vw_tab, v_words[0])
        vs_picked = keep.tile([P, V], U8, name="vs_picked", tag="xs_tab", align_bytes=64)
        nc.vector.tensor_copy(vs_picked[:], vs_tab[:].indirect(doc_t[:]))
        for r in range(ROWS):
            nc.sync.dma_start(out=vs[V_PLANE + r : P : QUAD, :].bitcast(I32), in_=vs_picked[V_FIRST + V_STEP * r : V_ROWS.stop : ROWS * V_STEP, :].bitcast(I32))

        xw = [keep.tile([P, S], U32, name="xw%d" % o, align_bytes=64) for o in range(PASSES)]

        def pick(dst, tab, lst, lo, hi):
            nc.vector.tensor_copy(dst, tab[:].bitcast(U32).indirect(lst[:, lo // LIST : hi // LIST]))

        def pick_words(o, cuts):
            for lo, hi in zip(cuts, cuts[1:]):
                pick(xw[o][:, lo:hi], xw_tab[o], offs_t, lo, hi)

        w_codes, w_scales = [], []
        for o in range(PASSES):
            grouped = keep.tile([P, H * PACK], BF16, name="w_grouped%d" % o, align_bytes=64)
            dst = grouped[:].rearrange("p (t m j) -> p m j t", t=PACK, j=PACK)
            src = w_raw[o][:].rearrange("p j (m t) -> p m j t", t=PACK)
            nc.scalar.copy(dst, src)
            codes = keep.tile([P, H], U32, name="w_codes%d" % o, align_bytes=64)
            scales = keep.tile([P, H], U8, name="w_scales%d" % o, tag="vs_tab" if o == 0 else "xw_tab0", align_bytes=64)
            nc.vector.quantize_mx(out=codes[:].bitcast(FP8X4), scales=scales[:], in_=grouped[:])
            w_codes.append(codes)
            w_scales.append(scales)
            if o == 0:
                pick_words(0, (0, P, 2 * P, S))
        pick_words(1, (0, P, 2 * P, S))

        warm_bank = psum.tile([P, BANK], F32, name="bank3", tag="bank3")

        def warm_up(codes, scales):
            nc.tensor.matmul_mx(
                out=warm_bank[:WARM_M, :],
                lhsT=codes[:, :WARM_M].bitcast(FP8X4),
                lhsT_scale=scales[:, :WARM_M],
                rhs=w_codes[0][:].bitcast(FP8X4),
                rhs_scale=w_scales[0][:],
                start=True,
                stop=True,
            )

        for n in range(2):
            warm_up(w_codes[0], w_scales[0])

        h_bf = keep.tile([P, S * PACK], BF16, name="h_bf", align_bytes=64)
        h_codes, h_scales = [], []

        def bank(n):
            return psum.tile([P, BANK], F32, name="bank%d" % n, tag="bank%d" % n)

        accs = [bank(b) for b in range(BLOCKS - 1)]

        def project(o, b):
            for t in range(PACK):
                ch = slice(t * P, (t + 1) * P)
                nc.tensor.matmul_mx(
                    out=accs[b][:, ch],
                    lhsT=w_codes[o][:, ch].bitcast(FP8X4),
                    lhsT_scale=w_scales[o][:, ch],
                    rhs=xw[o][:, b * P : (b + 1) * P].bitcast(FP8X4),
                    rhs_scale=xs[:, o * S + b * P : o * S + (b + 1) * P],
                    start=(o == 0 and t == 0),
                    stop=(o == PASSES - 1 and t == PACK - 1),
                )

        for b in range(BLOCKS - 1):
            project(0, b)
        for b in range(BLOCKS):
            if b == BLOCKS - 1:
                accs.append(bank(0))
                project(0, b)
            project(1, b)
            block = h_bf[:, b * K_PASS : (b + 1) * K_PASS]
            nc.scalar.activation(
                block.rearrange("p (n t) -> p n t", t=PACK), accs[b][:].rearrange("p (t n) -> p n t", t=PACK), GELU
            )
            h_codes.append(keep.tile([P, P], U32, name="h_codes%d" % b, align_bytes=64))
            h_scales.append(keep.tile([P, P], U8, name="h_scales%d" % b, align_bytes=64))
            nc.vector.quantize_mx(out=h_codes[b][:].bitcast(FP8X4), scales=h_scales[b][:], in_=block)
        for b in (BLOCKS - 2, BLOCKS - 2, BLOCKS - 1, BLOCKS - 1):
            warm_up(h_codes[b], h_scales[b])

        vw = [keep.tile([P, BANK], U32, name="vw%d" % g, tag="vw%d" % g, align_bytes=64) for g in range(V // BANK)]
        for g in range(V // BANK):
            pick(vw[g][:], vw_tab, doc_t, g * BANK, (g + 1) * BANK)

        docs = BANK // D
        parts = [range(1, 3), range(3, 4)]
        quads = keep.tile([P, BLOCKS - 1, 4, R], F32, name="quads", tag="quads", align_bytes=64)
        pairs = [keep.tile([P, len(part), 2, R], F32, name="pairs%d" % n, tag="vw0" if n == 0 else "pairs1", align_bytes=64) for n, part in enumerate(parts)]
        best = [keep.tile([P, len(part), R], F32, name="best%d" % n, align_bytes=64) for n, part in enumerate(parts)]

        banks = {}

        def score_pass(g, b):
            banks[(g, b)] = bank(BLOCKS * (1 - g) + b)
            nc.tensor.matmul_mx(
                out=banks[(g, b)][:],
                lhsT=h_codes[b][:].bitcast(FP8X4),
                lhsT_scale=h_scales[b][:],
                rhs=vw[g][:].bitcast(FP8X4),
                rhs_scale=vs[V_PLANE:P, g * BANK : (g + 1) * BANK],
                start=True,
                stop=True,
            )

        def scores_of(g, b):
            return banks[(g, b)][:].rearrange("p (v d) -> p v d", d=D)

        def reduce_whole(g, b, tag):
            whole = keep.tile([P, docs], F32, name="whole%d" % g, tag=tag, align_bytes=64)
            nc.vector.tensor_reduce(whole[:], scores_of(g, b), AXIS_X, MAX)
            nc.sync.dma_start(out=out[b * P : (b + 1) * P, g * docs : (g + 1) * docs], in_=whole[:])

        def reduce_half(g, b):
            scores = banks[(g, b)][:].rearrange("p (v d) -> p d v", d=D)
            upper = keep.tile([P, 4, docs], F32, name="upper%d_%d" % (g, b), align_bytes=64)
            nc.scalar.copy(upper[:], scores[:, 4:, :])
            nc.vector.tensor_tensor(quads[:, b - 1, :, g * docs : (g + 1) * docs], scores[:, :4, :], upper[:], MAX)

        def halve(n, cols):
            mine = quads[:, parts[n].start - 1 : parts[n].stop - 1, :, cols]
            nc.vector.tensor_tensor(pairs[n][:, :, :, cols], mine[:, :, :2, :], mine[:, :, 2:, :], MAX)

        for b in range(BLOCKS):
            score_pass(0, b)
        reduce_whole(0, 0, "whole0")
        for b in range(1, BLOCKS):
            reduce_half(0, b)
        halve(0, slice(0, docs))
        for b in range(1, BLOCKS):
            score_pass(1, b)
            reduce_half(1, b)
        score_pass(1, 0)
        halve(0, slice(docs, R))
        halve(1, slice(0, R))
        for n, part in enumerate(parts):
            nc.vector.tensor_tensor(best[n][:], pairs[n][:, :, 0, :], pairs[n][:, :, 1, :], MAX)
            for b in part:
                nc.sync.dma_start(out=out[b * P : (b + 1) * P, :], in_=best[n][:, b - part.start, :])
        reduce_whole(1, 0, "quads")
